import numpy as np
import ml_dtypes


def mxq(x, axis, fmt="e4m3"):
    dtype, down = {"e4m3": (ml_dtypes.float8_e4m3fn, 7), "e5m2": (ml_dtypes.float8_e5m2, 14)}[fmt]
    v = np.moveaxis(np.asarray(x, np.float32).astype(ml_dtypes.bfloat16).astype(np.float64), axis, -1)
    blocks = v.reshape(v.shape[:-1] + (-1, 32))
    amax = np.abs(blocks).max(-1, keepdims=True)
    byte = np.maximum(np.where(amax > 0, np.frexp(amax)[1] - 1 + 127, 0) - down, 1)
    scale = np.exp2(byte - 127.0)
    codes = (blocks / scale).astype(np.float32).astype(dtype).astype(np.float64)
    return np.moveaxis((codes * scale).reshape(v.shape), -1, axis)


WIDE = False


def mx_kscale(k):
    if not WIDE:
        return np.ones(k)
    levels = np.array([10, -10, 5, -5, 0])
    if k % 512:
        return np.exp2(np.random.permutation(np.resize(levels, k // 32))).repeat(32)
    a = np.empty((k // 512, 16))
    for p in range(k // 512):
        a[p, :8] = np.random.permutation(np.resize(levels, 8))
        for g in range(8):
            far = levels[np.abs(levels - a[p, g]) >= 10]
            a[p, g + 8] = far[np.random.randint(len(far))]
    return np.exp2(a.ravel()).repeat(32)


def f64(x):
    return np.asarray(x).astype(np.float64)


def striped(idx):
    return np.tile(idx.reshape(-1, 16).T, (8, 1)).astype(np.uint16)


def unstriped(offs):
    return offs[:16].T.reshape(-1).astype(np.int64)


E2M1 = np.array([0.0, 0.5, 1.0, 1.5, 2.0, 3.0, 4.0, 6.0, -0.0, -0.5, -1.0, -1.5, -2.0, -3.0, -4.0, -6.0])


def pack_weight(w, fmt):
    k, n = w.shape
    w = f64(np.asarray(w, np.float32).astype(ml_dtypes.bfloat16)).reshape(k // 32, 32, n)
    amax = np.abs(w).max(1)
    if fmt == "e4m3":
        byte = np.frexp(amax)[1] - 1 + 127 - 7
    else:
        mant, ex = np.frexp(amax / 6.0)
        byte = np.where(mant > 0.5, ex, ex - 1) + 127
    byte = np.clip(np.where(amax > 0, byte, 1), 1, 254)
    scaled = (w * np.exp2(127.0 - byte)[:, None, :]).reshape(k, n).astype(np.float32)
    by_word = np.ascontiguousarray(scaled.reshape(k // 512, 128, 4, n).transpose(0, 1, 3, 2))
    if fmt == "e4m3":
        words = by_word.astype(ml_dtypes.float8_e4m3fn).view(np.uint8)
    else:
        c = by_word.astype(ml_dtypes.float4_e2m1fn).view(np.uint8) & 0xF
        words = (c[..., 0::2] | (c[..., 1::2] << 4)).reshape(k // 512, 128, 2 * n)
    return np.ascontiguousarray(words), np.ascontiguousarray(byte.astype(np.uint8).reshape(k // 512, 16, n))


def unpack_weight(words, scales, fmt):
    g, _, n = scales.shape
    words = np.ascontiguousarray(words).reshape(g, 128, n, -1)
    if fmt == "e4m3":
        vals = words.view(ml_dtypes.float8_e4m3fn).astype(np.float64)
    else:
        nib = np.empty((g, 128, n, 4), np.uint8)
        nib[..., 0::2] = words & 0xF
        nib[..., 1::2] = words >> 4
        vals = E2M1[nib]
    vals = vals * np.repeat(np.exp2(scales.astype(np.float64) - 127.0), 8, axis=1)[..., None]
    return vals.transpose(0, 1, 3, 2).reshape(g * 512, n)


def gelu(v):
    return 0.5 * v * (1.0 + np.tanh(np.sqrt(2.0 / np.pi) * (v + 0.044715 * v**3)))


K, T, S, M, N = 1536, 2048, 1024, 512, 1536

def setup_inputs():
    n = np.random.standard_normal
    s = mx_kscale(K)[:, None]
    u = mx_kscale(S)
    idx = np.random.permutation(T)[:S]
    tab_words, tab_scales = pack_weight(n((K, T)) * s / np.sqrt(K), "e4m3")
    w4_words, w4_scales = pack_weight(n((K, N)) * s / np.sqrt(K), "e2m1")
    wdT = n((N, T)) / np.sqrt(S)
    wdT[:, idx] /= u
    return {
        "tab_words": tab_words, "tab_scales": tab_scales,
        "offs": striped(idx),
        "x": (n((K, M)) / s).astype(np.float32),
        "b": (0.5 * n(S)).astype(np.float32),
        "g": (np.exp(0.3 * n(S)) * u).astype(np.float32),
        "wdT": wdT.astype(np.float32),
        "w4_words": w4_words, "w4_scales": w4_scales,
        "r": n((N, M)).astype(np.float32),
    }

def reference(tab_words, tab_scales, offs, x, b, g, wdT, w4_words, w4_scales, r):
    v = unpack_weight(tab_words, tab_scales, "e4m3")[:, unstriped(offs)]
    wd = f64(wdT)[:, unstriped(offs)]
    w4 = unpack_weight(w4_words, w4_scales, "e2m1")
    xq = mxq(f64(x), 0, "e4m3")
    score = v.T @ xq
    h = np.maximum(score + f64(b)[:, None], 0.0) * f64(g)[:, None]
    y = mxq(wd, 1, "e4m3") @ mxq(h, 0, "e4m3") + w4.T @ xq
    return y + f64(r)

@@ -1,0 +1,222 @@
+from contextlib import ExitStack
+
+import concourse.mybir as mybir
+from concourse.masks import make_identity
+
+K, T, S, M, N = 1536, 2048, 1024, 512, 1536
+FLOPS = 2 * M * (K * S + S * N + K * N)
+
+F32 = mybir.dt.float32
+BF16 = mybir.dt.bfloat16
+I32 = mybir.dt.int32
+U32 = mybir.dt.uint32
+U16 = mybir.dt.uint16
+U8 = mybir.dt.uint8
+FP8X4 = mybir.dt.float8_e4m3fn_x4
+FP4X4 = mybir.dt.float4_e2m1fn_x4
+ACT = mybir.ActivationFunctionType
+ALU = mybir.AluOpType
+
+P = 128
+KP = K // 512
+SP = S // 512
+KINDS = ["V","S","S","V","S","V"]
+LOADS = [["x",0],["w",0],["k",0],["s",0],["w",1],["x",1],["b",0],["k",1],["x",2],["k",2],["w",2],["w",3],["z",0],["d",0],["w",4],["w",5],["w",6],["w",7],["r",0],["w",8],["w",9],["w",10],["w",11],["r",1],["r",2]]
+X_ON = "S"
+RAW_BUFS = 8
+
+
+def tile_list_paged_memory_layer_kernel(tc, tab_words, tab_scales, offs, x, b, g, wdT, w4_words, w4_scales, r, out):
+    nc = tc.nc
+    with ExitStack() as ctx:
+        keep = ctx.enter_context(tc.tile_pool(name="keep", bufs=1))
+        ring = ctx.enter_context(tc.tile_pool(name="ring", bufs=2))
+        psum = ctx.enter_context(tc.psum_pool(name="psum", bufs=1))
+
+        offsets = keep.tile([P, S // 16], U16, name="offsets")
+        nc.sync.dma_start(offsets[:], offs)
+
+        key_scales = keep.tile([P, T], U8, name="key_scales", align_bytes=64)
+        nc.vector.memset(key_scales[:].bitcast(I32), 0)
+        bg_rows = keep.tile([P, SP * P], F32, name="bg_rows")
+        nc.vector.memset(bg_rows[:], 0.0)
+        dense_scales = keep.tile([P, KP, N], U8, name="dense_scales", align_bytes=64)
+        nc.vector.memset(dense_scales[:].rearrange("p a n -> p (a n)").bitcast(I32), 0)
+        ident = keep.tile([P, P], F32, name="ident")
+        make_identity(nc, ident[:])
+
+        warm = keep.tile([P, 8], F32, name="warm")
+        nc.vector.memset(warm[:, 0:1], 0.0)
+        nc.scalar.activation(warm[:, 4:5], warm[:, 0:1], ACT.Relu)
+
+        x_raw, keys, wd_raw, res = {}, {}, {}, {}
+        dense = keep.tile([P, KP, 2 * N], U8, name="dense", align_bytes=64)
+        for what, i in LOADS:
+            if what == "x":
+                x_raw[i] = ring.tile([P, 4, M], F32, name="x_raw", tag="xr", bufs=3)
+                nc.sync.dma_start(x_raw[i][:], x[512 * i : 512 * (i + 1), :].rearrange("(p t) m -> p t m", t=4))
+            elif what == "k":
+                keys[i] = keep.tile([P, T], I32, name="keys%d" % i)
+                nc.sync.dma_start(keys[i][:], tab_words[i].rearrange("p n t -> p (n t)").bitcast(I32))
+            elif what == "s":
+                for q in range(4):
+                    nc.sync.dma_start(key_scales[32 * q : 32 * q + 4 * KP, :].bitcast(I32), tab_scales[:, 4 * q : 4 * q + 4, :].bitcast(I32))
+            elif what == "b":
+                for i, vec in enumerate((b, g)):
+                    nc.sync.dma_start(bg_rows[4 * i : 4 * i + 4, :].rearrange("t (q r) -> t q r", r=8), vec.rearrange("(q t r) -> t q r", t=4, r=8))
+            elif what == "z":
+                for q in range(4):
+                    nc.sync.dma_start(dense_scales[32 * q : 32 * q + 4, :, :].bitcast(I32), w4_scales[:, 4 * q : 4 * q + 4, :].rearrange("a r n -> r a n").bitcast(I32))
+            elif what == "d":
+                nc.sync.dma_start(dense[:].bitcast(I32), w4_words.rearrange("a p n -> p a n").bitcast(I32))
+            elif what == "w":
+                pair, half = divmod(i, 2)
+                wd_raw[i] = ring.tile([P, T], F32, name="wd_raw", tag="wd_raw", bufs=RAW_BUFS)
+                if KINDS[pair] == "S":
+                    rows = wdT[256 * pair : 256 * (pair + 1), 1024 * half : 1024 * (half + 1)]
+                    nc.sync.dma_start(wd_raw[i][:].rearrange("p (e c) -> p e c", e=2), rows.rearrange("(p e) c -> p e c", e=2))
+                else:
+                    nc.sync.dma_start(wd_raw[i][:], wdT[P * i : P * (i + 1), :])
+            else:
+                res[i] = ring.tile([P, 4, M], F32, name="res", tag="xr", bufs=3)
+                nc.sync.dma_start(res[i][:], r[512 * i : 512 * (i + 1), :].rearrange("(i p) m -> p i m", p=P))
+
+        x_codes, x_scales, picked = {}, {}, {}
+        wq = {}
+
+        def quantise(src, name):
+            width = src.shape[1] // 4
+            codes = keep.tile([P, width], U32, name=name + "_codes", align_bytes=64)
+            scales = keep.tile([P, width], U8, name=name + "_scales", align_bytes=64)
+            nc.vector.quantize_mx(out=codes[:].bitcast(FP8X4), scales=scales[:], in_=src)
+            return codes, scales
+
+        def x_stage(a):
+            woven = ring.tile([P, 4 * M], BF16, name="woven", tag="woven", bufs=3, align_bytes=64)
+            dst = woven[:].rearrange("p (c i t) -> p c t i", i=4, t=4)
+            src = x_raw[a][:].rearrange("p t (c i) -> p c t i", i=4)
+            if X_ON == "S":
+                nc.scalar.copy(dst, src)
+            else:
+                nc.vector.tensor_copy(dst, src)
+            x_codes[a], x_scales[a] = quantise(woven[:], "x%d" % a)
+
+        def key_stage(a):
+            picked[a] = keep.tile([P, S], U32, name="picked%d" % a, align_bytes=64)
+            nc.vector.tensor_copy(picked[a][:].rearrange("p (t q r) -> p q t r", t=4, r=8), keys[a][:].bitcast(U32).indirect(offsets[:]))
+
+        def value_stage(pair):
+            if KINDS[pair] == "S":
+                words = ring.tile([P, 2 * T], BF16, name="words", tag="words", bufs=2)
+                for half in range(2):
+                    nc.scalar.copy(
+                        words[:, T * half : T * (half + 1)].rearrange("p (c e) -> p c e", e=2),
+                        wd_raw[2 * pair + half][:].rearrange("p (e c) -> p c e", e=2),
+                    )
+                got = ring.tile([P, S], U32, name="got", tag="got", bufs=2)
+                nc.vector.tensor_copy(got[:].rearrange("p (t q r) -> p q t r", t=4, r=8), words[:].bitcast(U32).indirect(offsets[:]))
+                for a in range(SP):
+                    bank = psum.tile([P, 4, P], F32, name="turned", tag="turned", bufs=3)
+                    for t in range(4):
+                        nc.tensor.transpose(bank[:, t, :], got[:, 256 * t + P * a : 256 * t + P * (a + 1)].bitcast(F32), ident[:])
+                    wb = ring.tile([P, 1024], BF16, name="wb", tag="wb", bufs=4, align_bytes=64)
+                    nc.scalar.copy(wb[:].rearrange("p (c t) -> p c t", t=4), bank[:].rearrange("p t n -> p (t n)").bitcast(BF16).rearrange("p (t c) -> p c t", t=4))
+                    codes, scales = quantise(wb[:], "w%d_%d" % (pair, a))
+                    for h in range(2):
+                        wq[(2 * pair + h, a)] = (codes[:, P * h : P * (h + 1)], scales[:, P * h : P * (h + 1)])
+            else:
+                for h in range(2):
+                    i = 2 * pair + h
+                    got = ring.tile([P, S], BF16, name="gotv", tag="gotv", bufs=2)
+                    nc.vector.tensor_copy(got[:].rearrange("p (u q r e) -> p q u e r", u=2, r=8, e=2), wd_raw[i][:].indirect(offsets[:]))
+                    bank = psum.tile([P, SP, 2, P], F32, name="turned", tag="turned", bufs=3)
+                    got_words = got[:].bitcast(F32)
+                    for a in range(SP):
+                        for u in range(2):
+                            nc.tensor.transpose(bank[:, a, u, :], got_words[:, 256 * u + P * a : 256 * u + P * (a + 1)], ident[:])
+                    wb = ring.tile([P, 1024], BF16, name="wb", tag="wb", bufs=4, align_bytes=64)
+                    nc.scalar.copy(wb[:].bitcast(F32).rearrange("p (a n u) -> p a n u", a=SP, u=2), bank[:].rearrange("p a u n -> p a n u"))
+                    codes, scales = quantise(wb[:], "w%d_%d" % (pair, h))
+                    for a in range(SP):
+                        wq[(i, a)] = (codes[:, P * a : P * (a + 1)], scales[:, P * a : P * (a + 1)])
+
+        h_q = {}
+
+        def score_stage():
+            for a in range(SP):
+                act = ring.tile([P, 4, M], F32, name="act", tag="act", bufs=2)
+                for t in range(4):
+                    bank = psum.tile([P, M], F32, name="acc", tag="acc", bufs=5)
+                    cols = slice(256 * t + P * a, 256 * t + P * (a + 1))
+                    for k in range(KP):
+                        nc.tensor.matmul_mx(
+                            out=bank[:],
+                            lhsT=picked[k][:, cols].bitcast(FP8X4),
+                            lhsT_scale=picked_scales[4 * k : P, cols],
+                            rhs=x_codes[k][:].bitcast(FP8X4),
+                            rhs_scale=x_scales[k][:],
+                            start=(k == 0),
+                            stop=(k == KP - 1),
+                        )
+                    nc.scalar.activation(act[:, t, :], bank[:], ACT.Relu, bias=bg[:, a, t : t + 1])
+                woven = ring.tile([P, 4 * M], BF16, name="woven", tag="woven", bufs=3, align_bytes=64)
+                nc.vector.tensor_tensor(
+                    woven[:].rearrange("p (c i t) -> p c t i", i=4, t=4),
+                    act[:].rearrange("p t (c i) -> p c t i", i=4),
+                    bg[:, a, 4:8].unsqueeze(1).unsqueeze(3).to_broadcast([P, M // 4, 4, 4]),
+                    ALU.mult,
+                )
+                h_q[a] = quantise(woven[:], "h%d" % a)
+
+        def out_stage(i):
+            bank = psum.tile([P, M], F32, name="acc", tag="acc", bufs=5)
+            for k in range(KP):
+                nc.tensor.matmul_mx(
+                    out=bank[:],
+                    lhsT=dense[:, k, 2 * P * i : 2 * P * (i + 1)].bitcast(FP4X4),
+                    lhsT_scale=dense_scales[:, k, P * i : P * (i + 1)],
+                    rhs=x_codes[k][:].bitcast(FP8X4),
+                    rhs_scale=x_scales[k][:],
+                    start=(k == 0),
+                    stop=False,
+                )
+            for a in range(SP):
+                nc.tensor.matmul_mx(
+                    out=bank[:],
+                    lhsT=wq[(i, a)][0].bitcast(FP8X4),
+                    lhsT_scale=wq[(i, a)][1],
+                    rhs=h_q[a][0][:].bitcast(FP8X4),
+                    rhs_scale=h_q[a][1][:],
+                    start=False,
+                    stop=(a == SP - 1),
+                )
+            mine = res[i // 4][:, i % 4, :]
+            nc.vector.tensor_tensor(mine, bank[:], mine, ALU.add)
+
+        bg = keep.tile([P, SP, 8], F32, name="bg")
+        bank = psum.tile([P, SP, P], F32, name="turned", tag="turned", bufs=3)
+        for a in range(SP):
+            nc.tensor.transpose(bank[:, a, :], bg_rows[:, P * a : P * (a + 1)], ident[:])
+        nc.scalar.copy(bg[:], bank[:, :, 0:8])
+
+        listed_scales = keep.tile([P, S], U8, name="listed_scales", align_bytes=64)
+        nc.vector.tensor_copy(listed_scales[:], key_scales[:].indirect(offsets[:]))
+        picked_scales = keep.tile([P, S], U8, name="picked_scales", align_bytes=64)
+        nc.vector.tensor_copy(
+            picked_scales[:].bitcast(I32).rearrange("p (t q w) -> p t q w", t=4, w=2),
+            listed_scales[:].bitcast(I32).rearrange("p (q t w) -> p t q w", t=4, w=2),
+        )
+        for what, i in [["x",0],["k",0],["w",0],["x",1],["k",1],["x",2],["k",2],["h",0],["w",1],["o",0],["w",2],["o",1],["w",3],["o",2],["w",4],["o",3],["w",5],["o",4],["o",5]]:
+            if what == "x":
+                x_stage(i)
+            elif what == "k":
+                key_stage(i)
+            elif what == "w":
+                value_stage(i)
+            elif what == "h":
+                score_stage()
+            else:
+                out_stage(2 * i)
+                out_stage(2 * i + 1)
+        for i in range(N // P):
+            nc.sync.dma_start(out[P * i : P * (i + 1), :], res[i // 4][:, i % 4, :])

@@ -20,40 +20,50 @@ ALU = mybir.AluOpType
 P = 128
 KP = K // 512
 SP = S // 512
-KINDS = ["V","S","S","V","S","V"]
-LOADS = [["x",0],["w",0],["k",0],["s",0],["w",1],["x",1],["b",0],["k",1],["x",2],["k",2],["w",2],["w",3],["z",0],["d",0],["w",4],["w",5],["w",6],["w",7],["r",0],["w",8],["w",9],["w",10],["w",11],["r",1],["r",2]]
-X_ON = "S"
-RAW_BUFS = 8
+SLOT = 8192
+LOADS = [["s",0],["b",0],["x",0],["w",0],["k",0],["w",1],["x",1],["k",1],["x",2],["k",2],["w",2],["w",3],["w",4],["w",5],["z",0],["d",0],["w",6],["w",7],["r",0],["w",8],["w",9],["w",10],["w",11],["r",1],["r",2]]
+WORK = [["b",0],["s",0],["x",0],["k",0],["c",0],["c",1],["g",0],["x",1],["k",1],["x",2],["k",2],["c",2],["C",3],["g",1],["h",0],["m",0],["h",1],["m",1],["n",0],["n",1],["q",0],["q",1],["c",4],["c",5],["g",2],["q",2],["q",3],["y",0],["a",0],["y",1],["a",1],["c",6],["C",7],["g",3],["q",4],["q",5],["y",2],["a",2],["y",3],["a",3],["c",8],["c",9],["g",4],["q",6],["q",7],["c",10],["C",11],["g",5],["y",4],["a",4],["y",5],["a",5],["q",8],["q",9],["y",6],["a",6],["y",7],["a",7],["y",8],["a",8],["y",9],["a",9],["q",10],["q",11],["y",10],["a",10],["y",11],["a",11]]
+X_ON = "SSS"
+PLACE = {"raw0":[0,0],"raw1":[1,0],"raw2":[2,0],"raw3":[3,0],"raw4":[4,0],"raw5":[5,0],"raw6":[6,0],"raw7":[7,0],"raw8":[8,0],"raw9":[9,0],"raw10":[10,0],"raw11":[11,0],"x0":[13,0],"r0":[13,0],"x1":[14,0],"r1":[14,0],"x2":[15,0],"r2":[15,0],"words0":[12,0],"words1":[0,0],"words2":[3,0],"words3":[2,0],"words4":[1,0],"words5":[4,0],"act0":[2,0],"act1":[1,0],"hw0":[0,0],"wb0_0":[15,0],"wb0_1":[15,2048],"wb1_0":[5,0],"wb1_1":[5,2048],"wb2_0":[6,0],"wb2_1":[6,2048],"wb3_0":[9,0],"wb3_1":[9,2048],"wb4_0":[10,0],"wb4_1":[10,2048],"wb5_0":[7,0],"wb5_1":[7,2048],"out2":[2,0],"out3":[2,2048],"out4":[1,0],"out5":[1,2048],"out6":[4,0],"out7":[4,2048]}
 
 
 def tile_list_paged_memory_layer_kernel(tc, tab_words, tab_scales, offs, x, b, g, wdT, w4_words, w4_scales, r, out):
     nc = tc.nc
     with ExitStack() as ctx:
         keep = ctx.enter_context(tc.tile_pool(name="keep", bufs=1))
+        arena = ctx.enter_context(tc.tile_pool(name="arena", bufs=1))
         ring = ctx.enter_context(tc.tile_pool(name="ring", bufs=2))
         psum = ctx.enter_context(tc.psum_pool(name="psum", bufs=1))
+
+        def placed(name, shape, dtype):
+            slot, at = PLACE[name]
+            return arena.tile(shape, dtype, name=name, offset=SLOT * slot + at, align_bytes=64)
 
         offsets = keep.tile([P, S // 16], U16, name="offsets")
         nc.sync.dma_start(offsets[:], offs)
 
         key_scales = keep.tile([P, T], U8, name="key_scales", align_bytes=64)
-        nc.vector.memset(key_scales[:].bitcast(I32), 0)
+        nc.gpsimd.memset(key_scales[:].bitcast(I32), 0)
         bg_rows = keep.tile([P, SP * P], F32, name="bg_rows")
-        nc.vector.memset(bg_rows[:], 0.0)
+        nc.gpsimd.memset(bg_rows[:], 0.0)
         dense_scales = keep.tile([P, KP, N], U8, name="dense_scales", align_bytes=64)
         nc.vector.memset(dense_scales[:].rearrange("p a n -> p (a n)").bitcast(I32), 0)
         ident = keep.tile([P, P], F32, name="ident")
         make_identity(nc, ident[:])
 
         warm = keep.tile([P, 8], F32, name="warm")
-        nc.vector.memset(warm[:, 0:1], 0.0)
-        nc.scalar.activation(warm[:, 4:5], warm[:, 0:1], ACT.Relu)
+        nc.scalar.activation(warm[:, 0:1], ident[:, 0:1], ACT.Relu)
 
         x_raw, keys, wd_raw, res = {}, {}, {}, {}
         dense = keep.tile([P, KP, 2 * N], U8, name="dense", align_bytes=64)
-        for what, i in LOADS:
+        bg = keep.tile([P, SP, 8], F32, name="bg")
+        picked_scales = keep.tile([P, S], U8, name="picked_scales", align_bytes=64)
+        x_q, picked, wq, h_q = {}, {}, {}, {}
+        words, acts, wovens, turned, banks, results = {}, {}, {}, {}, {}, {}
+
+        def load(what, i):
             if what == "x":
-                x_raw[i] = ring.tile([P, 4, M], F32, name="x_raw", tag="xr", bufs=3)
+                x_raw[i] = placed("x%d" % i, [P, 4, M], F32)
                 nc.sync.dma_start(x_raw[i][:], x[512 * i : 512 * (i + 1), :].rearrange("(p t) m -> p t m", t=4))
             elif what == "k":
                 keys[i] = keep.tile([P, T], I32, name="keys%d" % i)
@@ -62,8 +72,8 @@ def tile_list_paged_memory_layer_kernel(tc, tab_words, tab_scales, offs, x, b, g
                 for q in range(4):
                     nc.sync.dma_start(key_scales[32 * q : 32 * q + 4 * KP, :].bitcast(I32), tab_scales[:, 4 * q : 4 * q + 4, :].bitcast(I32))
             elif what == "b":
-                for i, vec in enumerate((b, g)):
-                    nc.sync.dma_start(bg_rows[4 * i : 4 * i + 4, :].rearrange("t (q r) -> t q r", r=8), vec.rearrange("(q t r) -> t q r", t=4, r=8))
+                for j, vec in enumerate((b, g)):
+                    nc.sync.dma_start(bg_rows[4 * j : 4 * j + 4, :].rearrange("t (q r) -> t q r", r=8), vec.rearrange("(q t r) -> t q r", t=4, r=8))
             elif what == "z":
                 for q in range(4):
                     nc.sync.dma_start(dense_scales[32 * q : 32 * q + 4, :, :].bitcast(I32), w4_scales[:, 4 * q : 4 * q + 4, :].rearrange("a r n -> r a n").bitcast(I32))
@@ -71,152 +81,138 @@ def tile_list_paged_memory_layer_kernel(tc, tab_words, tab_scales, offs, x, b, g
                 nc.sync.dma_start(dense[:].bitcast(I32), w4_words.rearrange("a p n -> p a n").bitcast(I32))
             elif what == "w":
                 pair, half = divmod(i, 2)
-                wd_raw[i] = ring.tile([P, T], F32, name="wd_raw", tag="wd_raw", bufs=RAW_BUFS)
-                if KINDS[pair] == "S":
-                    rows = wdT[256 * pair : 256 * (pair + 1), 1024 * half : 1024 * (half + 1)]
-                    nc.sync.dma_start(wd_raw[i][:].rearrange("p (e c) -> p e c", e=2), rows.rearrange("(p e) c -> p e c", e=2))
-                else:
-                    nc.sync.dma_start(wd_raw[i][:], wdT[P * i : P * (i + 1), :])
+                wd_raw[i] = placed("raw%d" % i, [P, 2, T // 2], F32)
+                rows = wdT[256 * pair : 256 * (pair + 1), 1024 * half : 1024 * (half + 1)]
+                nc.sync.dma_start(wd_raw[i][:], rows.rearrange("(p e) c -> p e c", e=2))
             else:
-                res[i] = ring.tile([P, 4, M], F32, name="res", tag="xr", bufs=3)
+                res[i] = placed("r%d" % i, [P, 4, M], F32)
                 nc.sync.dma_start(res[i][:], r[512 * i : 512 * (i + 1), :].rearrange("(i p) m -> p i m", p=P))
-
-        x_codes, x_scales, picked = {}, {}, {}
-        wq = {}
 
         def quantise(src, name):
             width = src.shape[1] // 4
-            codes = keep.tile([P, width], U32, name=name + "_codes", align_bytes=64)
+            if name + "_codes" in PLACE:
+                codes = placed(name + "_codes", [P, width], U32)
+            else:
+                codes = keep.tile([P, width], U32, name=name + "_codes", align_bytes=64)
             scales = keep.tile([P, width], U8, name=name + "_scales", align_bytes=64)
             nc.vector.quantize_mx(out=codes[:].bitcast(FP8X4), scales=scales[:], in_=src)
             return codes, scales
 
-        def x_stage(a):
-            woven = ring.tile([P, 4 * M], BF16, name="woven", tag="woven", bufs=3, align_bytes=64)
-            dst = woven[:].rearrange("p (c i t) -> p c t i", i=4, t=4)
-            src = x_raw[a][:].rearrange("p t (c i) -> p c t i", i=4)
-            if X_ON == "S":
-                nc.scalar.copy(dst, src)
-            else:
-                nc.vector.tensor_copy(dst, src)
-            x_codes[a], x_scales[a] = quantise(woven[:], "x%d" % a)
+        def woven_tile(name):
+            if name in PLACE:
+                return placed(name, [P, 4 * M], BF16)
+            return ring.tile([P, 4 * M], BF16, name="woven", tag="woven", bufs=3, align_bytes=64)
 
-        def key_stage(a):
-            picked[a] = keep.tile([P, S], U32, name="picked%d" % a, align_bytes=64)
-            nc.vector.tensor_copy(picked[a][:].rearrange("p (t q r) -> p q t r", t=4, r=8), keys[a][:].bitcast(U32).indirect(offsets[:]))
-
-        def value_stage(pair):
-            if KINDS[pair] == "S":
-                words = ring.tile([P, 2 * T], BF16, name="words", tag="words", bufs=2)
-                for half in range(2):
-                    nc.scalar.copy(
-                        words[:, T * half : T * (half + 1)].rearrange("p (c e) -> p c e", e=2),
-                        wd_raw[2 * pair + half][:].rearrange("p (e c) -> p c e", e=2),
-                    )
+        def step(what, i):
+            if what == "b":
+                bank = psum.tile([P, SP, P], F32, name="turned", tag="turned", bufs=3)
+                for a in range(SP):
+                    nc.tensor.transpose(bank[:, a, :], bg_rows[:, P * a : P * (a + 1)], ident[:])
+                nc.scalar.copy(bg[:], bank[:, :, 0:8])
+            elif what == "s":
+                listed_scales = keep.tile([P, S], U8, name="listed_scales", align_bytes=64)
+                nc.vector.tensor_copy(listed_scales[:], key_scales[:].indirect(offsets[:]))
+                nc.vector.tensor_copy(
+                    picked_scales[:].bitcast(I32).rearrange("p (t q w) -> p t q w", t=4, w=2),
+                    listed_scales[:].bitcast(I32).rearrange("p (q t w) -> p t q w", t=4, w=2),
+                )
+            elif what == "x":
+                woven = woven_tile("xw%d" % i)
+                dst = woven[:].rearrange("p (c i t) -> p c t i", i=4, t=4)
+                src = x_raw[i][:].rearrange("p t (c i) -> p c t i", i=4)
+                if X_ON[i] == "S":
+                    nc.scalar.copy(dst, src)
+                else:
+                    nc.vector.tensor_copy(dst, src)
+                x_q[i] = quantise(woven[:], "x%d" % i)
+            elif what == "k":
+                picked[i] = keep.tile([P, S], U32, name="picked%d" % i, align_bytes=64)
+                nc.vector.tensor_copy(picked[i][:].rearrange("p (t q r) -> p q t r", t=4, r=8), keys[i][:].bitcast(U32).indirect(offsets[:]))
+            elif what == "c" or what == "C":
+                pair, half = divmod(i, 2)
+                if pair not in words:
+                    words[pair] = placed("words%d" % pair, [P, 2 * T], BF16)
+                dst = words[pair][:, T * half : T * (half + 1)].rearrange("p (c e) -> p c e", e=2)
+                src = wd_raw[i][:].rearrange("p e c -> p c e")
+                if what == "c":
+                    nc.scalar.copy(dst, src)
+                else:
+                    nc.vector.tensor_copy(dst, src)
+            elif what == "g":
                 got = ring.tile([P, S], U32, name="got", tag="got", bufs=2)
-                nc.vector.tensor_copy(got[:].rearrange("p (t q r) -> p q t r", t=4, r=8), words[:].bitcast(U32).indirect(offsets[:]))
+                nc.vector.tensor_copy(got[:].rearrange("p (t q r) -> p q t r", t=4, r=8), words[i][:].bitcast(U32).indirect(offsets[:]))
                 for a in range(SP):
                     bank = psum.tile([P, 4, P], F32, name="turned", tag="turned", bufs=3)
                     for t in range(4):
                         nc.tensor.transpose(bank[:, t, :], got[:, 256 * t + P * a : 256 * t + P * (a + 1)].bitcast(F32), ident[:])
-                    wb = ring.tile([P, 1024], BF16, name="wb", tag="wb", bufs=4, align_bytes=64)
+                    wb = placed("wb%d_%d" % (i, a), [P, 1024], BF16)
                     nc.scalar.copy(wb[:].rearrange("p (c t) -> p c t", t=4), bank[:].rearrange("p t n -> p (t n)").bitcast(BF16).rearrange("p (t c) -> p c t", t=4))
-                    codes, scales = quantise(wb[:], "w%d_%d" % (pair, a))
-                    for h in range(2):
-                        wq[(2 * pair + h, a)] = (codes[:, P * h : P * (h + 1)], scales[:, P * h : P * (h + 1)])
-            else:
+                    turned[2 * i + a] = wb
+            elif what == "q":
+                pair, a = divmod(i, 2)
+                codes, scales = quantise(turned[i][:], "w%d" % i)
                 for h in range(2):
-                    i = 2 * pair + h
-                    got = ring.tile([P, S], BF16, name="gotv", tag="gotv", bufs=2)
-                    nc.vector.tensor_copy(got[:].rearrange("p (u q r e) -> p q u e r", u=2, r=8, e=2), wd_raw[i][:].indirect(offsets[:]))
-                    bank = psum.tile([P, SP, 2, P], F32, name="turned", tag="turned", bufs=3)
-                    got_words = got[:].bitcast(F32)
-                    for a in range(SP):
-                        for u in range(2):
-                            nc.tensor.transpose(bank[:, a, u, :], got_words[:, 256 * u + P * a : 256 * u + P * (a + 1)], ident[:])
-                    wb = ring.tile([P, 1024], BF16, name="wb", tag="wb", bufs=4, align_bytes=64)
-                    nc.scalar.copy(wb[:].bitcast(F32).rearrange("p (a n u) -> p a n u", a=SP, u=2), bank[:].rearrange("p a u n -> p a n u"))
-                    codes, scales = quantise(wb[:], "w%d_%d" % (pair, h))
-                    for a in range(SP):
-                        wq[(i, a)] = (codes[:, P * a : P * (a + 1)], scales[:, P * a : P * (a + 1)])
-
-        h_q = {}
-
-        def score_stage():
-            for a in range(SP):
-                act = ring.tile([P, 4, M], F32, name="act", tag="act", bufs=2)
+                    wq[(2 * pair + h, a)] = (codes[:, P * h : P * (h + 1)], scales[:, P * h : P * (h + 1)])
+            elif what == "h":
+                acts[i] = placed("act%d" % i, [P, 4, M], F32)
                 for t in range(4):
                     bank = psum.tile([P, M], F32, name="acc", tag="acc", bufs=5)
-                    cols = slice(256 * t + P * a, 256 * t + P * (a + 1))
+                    cols = slice(256 * t + P * i, 256 * t + P * (i + 1))
                     for k in range(KP):
                         nc.tensor.matmul_mx(
                             out=bank[:],
                             lhsT=picked[k][:, cols].bitcast(FP8X4),
                             lhsT_scale=picked_scales[4 * k : P, cols],
-                            rhs=x_codes[k][:].bitcast(FP8X4),
-                            rhs_scale=x_scales[k][:],
+                            rhs=x_q[k][0][:].bitcast(FP8X4),
+                            rhs_scale=x_q[k][1][:],
                             start=(k == 0),
                             stop=(k == KP - 1),
                         )
-                    nc.scalar.activation(act[:, t, :], bank[:], ACT.Relu, bias=bg[:, a, t : t + 1])
-                woven = ring.tile([P, 4 * M], BF16, name="woven", tag="woven", bufs=3, align_bytes=64)
+                    nc.scalar.activation(acts[i][:, t, :], bank[:], ACT.Relu, bias=bg[:, i, t : t + 1])
+            elif what == "m":
+                wovens[i] = woven_tile("hw%d" % i)
                 nc.vector.tensor_tensor(
-                    woven[:].rearrange("p (c i t) -> p c t i", i=4, t=4),
-                    act[:].rearrange("p t (c i) -> p c t i", i=4),
-                    bg[:, a, 4:8].unsqueeze(1).unsqueeze(3).to_broadcast([P, M // 4, 4, 4]),
+                    wovens[i][:].rearrange("p (c i t) -> p c t i", i=4, t=4),
+                    acts[i][:].rearrange("p t (c i) -> p c t i", i=4),
+                    bg[:, i, 4:8].unsqueeze(1).unsqueeze(3).to_broadcast([P, M // 4, 4, 4]),
                     ALU.mult,
                 )
-                h_q[a] = quantise(woven[:], "h%d" % a)
-
-        def out_stage(i):
-            bank = psum.tile([P, M], F32, name="acc", tag="acc", bufs=5)
-            for k in range(KP):
-                nc.tensor.matmul_mx(
-                    out=bank[:],
-                    lhsT=dense[:, k, 2 * P * i : 2 * P * (i + 1)].bitcast(FP4X4),
-                    lhsT_scale=dense_scales[:, k, P * i : P * (i + 1)],
-                    rhs=x_codes[k][:].bitcast(FP8X4),
-                    rhs_scale=x_scales[k][:],
-                    start=(k == 0),
-                    stop=False,
-                )
-            for a in range(SP):
-                nc.tensor.matmul_mx(
-                    out=bank[:],
-                    lhsT=wq[(i, a)][0].bitcast(FP8X4),
-                    lhsT_scale=wq[(i, a)][1],
-                    rhs=h_q[a][0][:].bitcast(FP8X4),
-                    rhs_scale=h_q[a][1][:],
-                    start=False,
-                    stop=(a == SP - 1),
-                )
-            mine = res[i // 4][:, i % 4, :]
-            nc.vector.tensor_tensor(mine, bank[:], mine, ALU.add)
-
-        bg = keep.tile([P, SP, 8], F32, name="bg")
-        bank = psum.tile([P, SP, P], F32, name="turned", tag="turned", bufs=3)
-        for a in range(SP):
-            nc.tensor.transpose(bank[:, a, :], bg_rows[:, P * a : P * (a + 1)], ident[:])
-        nc.scalar.copy(bg[:], bank[:, :, 0:8])
-
-        listed_scales = keep.tile([P, S], U8, name="listed_scales", align_bytes=64)
-        nc.vector.tensor_copy(listed_scales[:], key_scales[:].indirect(offsets[:]))
-        picked_scales = keep.tile([P, S], U8, name="picked_scales", align_bytes=64)
-        nc.vector.tensor_copy(
-            picked_scales[:].bitcast(I32).rearrange("p (t q w) -> p t q w", t=4, w=2),
-            listed_scales[:].bitcast(I32).rearrange("p (q t w) -> p t q w", t=4, w=2),
-        )
-        for what, i in [["x",0],["k",0],["w",0],["x",1],["k",1],["x",2],["k",2],["h",0],["w",1],["o",0],["w",2],["o",1],["w",3],["o",2],["w",4],["o",3],["w",5],["o",4],["o",5]]:
-            if what == "x":
-                x_stage(i)
-            elif what == "k":
-                key_stage(i)
-            elif what == "w":
-                value_stage(i)
-            elif what == "h":
-                score_stage()
+            elif what == "n":
+                h_q[i] = quantise(wovens[i][:], "h%d" % i)
+            elif what == "y":
+                bank = psum.tile([P, M], F32, name="acc", tag="acc", bufs=5)
+                for k in range(KP):
+                    nc.tensor.matmul_mx(
+                        out=bank[:],
+                        lhsT=dense[:, k, 2 * P * i : 2 * P * (i + 1)].bitcast(FP4X4),
+                        lhsT_scale=dense_scales[:, k, P * i : P * (i + 1)],
+                        rhs=x_q[k][0][:].bitcast(FP8X4),
+                        rhs_scale=x_q[k][1][:],
+                        start=(k == 0),
+                        stop=False,
+                    )
+                for a in range(SP):
+                    nc.tensor.matmul_mx(
+                        out=bank[:],
+                        lhsT=wq[(i, a)][0].bitcast(FP8X4),
+                        lhsT_scale=wq[(i, a)][1],
+                        rhs=h_q[a][0][:].bitcast(FP8X4),
+                        rhs_scale=h_q[a][1][:],
+                        start=False,
+                        stop=(a == SP - 1),
+                    )
+                banks[i] = bank
             else:
-                out_stage(2 * i)
-                out_stage(2 * i + 1)
+                mine = res[i // 4][:, i % 4, :]
+                results[i] = placed("out%d" % i, [P, M], F32)[:] if "out%d" % i in PLACE else mine
+                nc.vector.tensor_tensor(results[i], banks[i][:], mine, ALU.add)
+
+        for what, i in LOADS:
+            if (what, i) != ("r", 2):
+                load(what, i)
+        for what, i in WORK:
+            if what == "y" and i == 0:
+                load("r", 2)
+            step(what, i)
         for i in range(N // P):
-            nc.sync.dma_start(out[P * i : P * (i + 1), :], res[i // 4][:, i % 4, :])
+            nc.sync.dma_start(out[P * i : P * (i + 1), :], results[i])

@@ -21,10 +21,10 @@ P = 128
 KP = K // 512
 SP = S // 512
 SLOT = 8192
-LOADS = [["s",0],["b",0],["x",0],["w",0],["k",0],["w",1],["x",1],["k",1],["x",2],["k",2],["w",2],["w",3],["w",4],["w",5],["z",0],["d",0],["w",6],["w",7],["r",0],["w",8],["w",9],["w",10],["w",11],["r",1],["r",2]]
-WORK = [["b",0],["s",0],["x",0],["k",0],["c",0],["c",1],["g",0],["x",1],["k",1],["x",2],["k",2],["c",2],["C",3],["g",1],["h",0],["m",0],["h",1],["m",1],["n",0],["n",1],["q",0],["q",1],["c",4],["c",5],["g",2],["q",2],["q",3],["y",0],["a",0],["y",1],["a",1],["c",6],["C",7],["g",3],["q",4],["q",5],["y",2],["a",2],["y",3],["a",3],["c",8],["c",9],["g",4],["q",6],["q",7],["c",10],["C",11],["g",5],["y",4],["a",4],["y",5],["a",5],["q",8],["q",9],["y",6],["a",6],["y",7],["a",7],["y",8],["a",8],["y",9],["a",9],["q",10],["q",11],["y",10],["a",10],["y",11],["a",11]]
+LOADS = [["s",0],["b",0],["w",0],["w",1],["x",0],["k",0],["x",1],["x",2],["k",1],["k",2],["w",2],["w",3],["w",4],["w",5],["z",0],["d",0],["w",6],["w",7],["r",0],["w",8],["w",9],["w",10],["w",11],["r",1],["r",2]]
+WORK = [["b",0],["s",0],["x",0],["k",0],["c",0],["c",1],["g",0],["x",1],["k",1],["x",2],["k",2],["c",2],["C",3],["g",1],["h",0],["m",0],["h",1],["m",1],["n",0],["n",1],["q",0],["q",1],["c",4],["C",5],["g",2],["q",2],["q",3],["y",0],["a",0],["y",1],["a",1],["c",6],["C",7],["g",3],["q",4],["q",5],["y",2],["a",2],["y",3],["a",3],["c",8],["c",9],["g",4],["q",6],["q",7],["y",4],["a",4],["y",5],["a",5],["c",10],["C",11],["g",5],["q",8],["q",9],["y",6],["a",6],["y",7],["a",7],["y",8],["a",8],["y",9],["a",9],["q",10],["q",11],["y",10],["a",10],["y",11],["a",11]]
 X_ON = "SSS"
-PLACE = {"raw0":[0,0],"raw1":[1,0],"raw2":[2,0],"raw3":[3,0],"raw4":[4,0],"raw5":[5,0],"raw6":[6,0],"raw7":[7,0],"raw8":[8,0],"raw9":[9,0],"raw10":[10,0],"raw11":[11,0],"x0":[13,0],"r0":[13,0],"x1":[14,0],"r1":[14,0],"x2":[15,0],"r2":[15,0],"words0":[12,0],"words1":[0,0],"words2":[3,0],"words3":[2,0],"words4":[1,0],"words5":[4,0],"act0":[2,0],"act1":[1,0],"hw0":[0,0],"wb0_0":[15,0],"wb0_1":[15,2048],"wb1_0":[5,0],"wb1_1":[5,2048],"wb2_0":[6,0],"wb2_1":[6,2048],"wb3_0":[9,0],"wb3_1":[9,2048],"wb4_0":[10,0],"wb4_1":[10,2048],"wb5_0":[7,0],"wb5_1":[7,2048],"out2":[2,0],"out3":[2,2048],"out4":[1,0],"out5":[1,2048],"out6":[4,0],"out7":[4,2048]}
+PLACE = {"raw0":[0,0],"raw1":[1,0],"raw2":[2,0],"raw3":[12,0],"raw4":[4,0],"raw5":[5,0],"raw6":[6,0],"raw7":[7,0],"raw8":[8,0],"raw9":[9,0],"raw10":[10,0],"raw11":[11,0],"x0":[13,0],"r0":[13,0],"x1":[14,0],"r1":[14,0],"x2":[15,0],"r2":[15,0],"words0":[3,0],"words1":[0,0],"words2":[12,0],"words3":[0,0],"words4":[12,0],"words5":[5,0],"act0":[2,64],"act1":[1,64],"wb0_0":[15,0],"wb0_1":[15,2048],"wb1_0":[4,0],"wb1_1":[4,2048],"wb2_0":[6,0],"wb2_1":[6,2048],"wb3_0":[9,0],"wb3_1":[9,2048],"wb4_0":[10,0],"wb4_1":[10,2048],"wb5_0":[7,0],"wb5_1":[7,2048]}
 
 
 def tile_list_paged_memory_layer_kernel(tc, tab_words, tab_scales, offs, x, b, g, wdT, w4_words, w4_scales, r, out):
@@ -146,7 +146,10 @@ def tile_list_paged_memory_layer_kernel(tc, tab_words, tab_scales, offs, x, b, g
                     for t in range(4):
                         nc.tensor.transpose(bank[:, t, :], got[:, 256 * t + P * a : 256 * t + P * (a + 1)].bitcast(F32), ident[:])
                     wb = placed("wb%d_%d" % (i, a), [P, 1024], BF16)
-                    nc.scalar.copy(wb[:].rearrange("p (c t) -> p c t", t=4), bank[:].rearrange("p t n -> p (t n)").bitcast(BF16).rearrange("p (t c) -> p c t", t=4))
+                    nc.scalar.copy(
+                        wb[:].rearrange("p (c i t) -> p c t i", i=4, t=4),
+                        bank[:].rearrange("p t n -> p (t n)").bitcast(BF16).rearrange("p (t c i) -> p c t i", t=4, i=4),
+                    )
                     turned[2 * i + a] = wb
             elif what == "q":
                 pair, a = divmod(i, 2)

@@ -18,13 +18,32 @@ ACT = mybir.ActivationFunctionType
 ALU = mybir.AluOpType
 
 P = 128
-KP = K // 512
-SP = S // 512
+PASS = 4 * P
+K_PASSES = K // PASS
+S_PASSES = S // PASS
+GROUP = 2 * P
+GROUPS = N // GROUP
+R_TILES = 4
+EARLY_GROUPS = 2
+VECTOR_EVERY = 3
+SUM_BANKS, TURN_BANKS = 6, 2
+
 SLOT = 8192
-LOADS = [["s",0],["b",0],["w",0],["w",1],["x",0],["k",0],["x",1],["x",2],["k",1],["k",2],["w",2],["w",3],["w",4],["w",5],["z",0],["d",0],["w",6],["w",7],["r",0],["w",8],["w",9],["w",10],["w",11],["r",1],["r",2]]
-WORK = [["b",0],["s",0],["x",0],["k",0],["c",0],["c",1],["g",0],["x",1],["k",1],["x",2],["k",2],["c",2],["C",3],["g",1],["h",0],["m",0],["h",1],["m",1],["n",0],["n",1],["q",0],["q",1],["c",4],["C",5],["g",2],["q",2],["q",3],["y",0],["a",0],["y",1],["a",1],["c",6],["C",7],["g",3],["q",4],["q",5],["y",2],["a",2],["y",3],["a",3],["c",8],["c",9],["g",4],["q",6],["q",7],["y",4],["a",4],["y",5],["a",5],["c",10],["C",11],["g",5],["q",8],["q",9],["y",6],["a",6],["y",7],["a",7],["y",8],["a",8],["y",9],["a",9],["q",10],["q",11],["y",10],["a",10],["y",11],["a",11]]
-X_ON = "SSS"
-PLACE = {"raw0":[0,0],"raw1":[1,0],"raw2":[2,0],"raw3":[12,0],"raw4":[4,0],"raw5":[5,0],"raw6":[6,0],"raw7":[7,0],"raw8":[8,0],"raw9":[9,0],"raw10":[10,0],"raw11":[11,0],"x0":[13,0],"r0":[13,0],"x1":[14,0],"r1":[14,0],"x2":[15,0],"r2":[15,0],"words0":[3,0],"words1":[0,0],"words2":[12,0],"words3":[0,0],"words4":[12,0],"words5":[5,0],"act0":[2,64],"act1":[1,64],"wb0_0":[15,0],"wb0_1":[15,2048],"wb1_0":[4,0],"wb1_1":[4,2048],"wb2_0":[6,0],"wb2_1":[6,2048],"wb3_0":[9,0],"wb3_1":[9,2048],"wb4_0":[10,0],"wb4_1":[10,2048],"wb5_0":[7,0],"wb5_1":[7,2048]}
+SPARE_SLOT = 2 * GROUPS
+TOKEN_SLOT = SPARE_SLOT + 1
+
+
+def on_vector(half):
+    return half % (2 * VECTOR_EVERY) == 2 * VECTOR_EVERY - 1
+
+
+def turned_slot(group):
+    if group == EARLY_GROUPS - 1:
+        return TOKEN_SLOT
+    if group == GROUPS - 1:
+        return 2 * EARLY_GROUPS
+    last = 2 * group + 3
+    return last - 1 if on_vector(last) else last
 
 
 def tile_list_paged_memory_layer_kernel(tc, tab_words, tab_scales, offs, x, b, g, wdT, w4_words, w4_scales, r, out):
@@ -35,8 +54,7 @@ def tile_list_paged_memory_layer_kernel(tc, tab_words, tab_scales, offs, x, b, g
         ring = ctx.enter_context(tc.tile_pool(name="ring", bufs=2))
         psum = ctx.enter_context(tc.psum_pool(name="psum", bufs=1))
 
-        def placed(name, shape, dtype):
-            slot, at = PLACE[name]
+        def placed(name, shape, dtype, slot, at=0):
             return arena.tile(shape, dtype, name=name, offset=SLOT * slot + at, align_bytes=64)
 
         offsets = keep.tile([P, S // 16], U16, name="offsets")
@@ -44,147 +62,127 @@ def tile_list_paged_memory_layer_kernel(tc, tab_words, tab_scales, offs, x, b, g
 
         key_scales = keep.tile([P, T], U8, name="key_scales", align_bytes=64)
         nc.gpsimd.memset(key_scales[:].bitcast(I32), 0)
-        bg_rows = keep.tile([P, SP * P], F32, name="bg_rows")
+        bg_rows = keep.tile([P, S_PASSES * P], F32, name="bg_rows")
         nc.gpsimd.memset(bg_rows[:], 0.0)
-        dense_scales = keep.tile([P, KP, N], U8, name="dense_scales", align_bytes=64)
+        dense_scales = keep.tile([P, K_PASSES, N], U8, name="dense_scales", align_bytes=64)
         nc.vector.memset(dense_scales[:].rearrange("p a n -> p (a n)").bitcast(I32), 0)
         ident = keep.tile([P, P], F32, name="ident")
         make_identity(nc, ident[:])
-
-        warm = keep.tile([P, 8], F32, name="warm")
-        nc.scalar.activation(warm[:, 0:1], ident[:, 0:1], ACT.Relu)
-
-        x_raw, keys, wd_raw, res = {}, {}, {}, {}
-        dense = keep.tile([P, KP, 2 * N], U8, name="dense", align_bytes=64)
-        bg = keep.tile([P, SP, 8], F32, name="bg")
+        dense = keep.tile([P, K_PASSES, 2 * N], U8, name="dense", align_bytes=64)
+        bg = keep.tile([P, S_PASSES, 8], F32, name="bg")
         picked_scales = keep.tile([P, S], U8, name="picked_scales", align_bytes=64)
-        x_q, picked, wq, h_q = {}, {}, {}, {}
-        words, acts, wovens, turned, banks, results = {}, {}, {}, {}, {}, {}
+        tokens, keys, halves, residual = {}, {}, {}, {}
+        x_q, picked, turned, values_q, woven_h, h_q, results = {}, {}, {}, {}, {}, {}, {}
 
-        def load(what, i):
-            if what == "x":
-                x_raw[i] = placed("x%d" % i, [P, 4, M], F32)
-                nc.sync.dma_start(x_raw[i][:], x[512 * i : 512 * (i + 1), :].rearrange("(p t) m -> p t m", t=4))
-            elif what == "k":
-                keys[i] = keep.tile([P, T], I32, name="keys%d" % i)
-                nc.sync.dma_start(keys[i][:], tab_words[i].rearrange("p n t -> p (n t)").bitcast(I32))
-            elif what == "s":
-                for q in range(4):
-                    nc.sync.dma_start(key_scales[32 * q : 32 * q + 4 * KP, :].bitcast(I32), tab_scales[:, 4 * q : 4 * q + 4, :].bitcast(I32))
-            elif what == "b":
-                for j, vec in enumerate((b, g)):
-                    nc.sync.dma_start(bg_rows[4 * j : 4 * j + 4, :].rearrange("t (q r) -> t q r", r=8), vec.rearrange("(q t r) -> t q r", t=4, r=8))
-            elif what == "z":
-                for q in range(4):
-                    nc.sync.dma_start(dense_scales[32 * q : 32 * q + 4, :, :].bitcast(I32), w4_scales[:, 4 * q : 4 * q + 4, :].rearrange("a r n -> r a n").bitcast(I32))
-            elif what == "d":
-                nc.sync.dma_start(dense[:].bitcast(I32), w4_words.rearrange("a p n -> p a n").bitcast(I32))
-            elif what == "w":
-                pair, half = divmod(i, 2)
-                wd_raw[i] = placed("raw%d" % i, [P, 2, T // 2], F32)
-                rows = wdT[256 * pair : 256 * (pair + 1), 1024 * half : 1024 * (half + 1)]
-                nc.sync.dma_start(wd_raw[i][:], rows.rearrange("(p e) c -> p e c", e=2))
-            else:
-                res[i] = placed("r%d" % i, [P, 4, M], F32)
-                nc.sync.dma_start(res[i][:], r[512 * i : 512 * (i + 1), :].rearrange("(i p) m -> p i m", p=P))
+        def load_halves(first, stop):
+            for half in range(first, stop):
+                group, side = divmod(half, 2)
+                halves[half] = placed("half%d" % half, [P, 2, T // 2], F32, half)
+                rows = wdT[GROUP * group : GROUP * (group + 1), T // 2 * side : T // 2 * (side + 1)]
+                nc.sync.dma_start(halves[half][:], rows.rearrange("(p e) c -> p e c", e=2))
+
+        def load_residual(j):
+            residual[j] = placed("residual%d" % j, [P, R_TILES, M], F32, TOKEN_SLOT + (j + 1) % K_PASSES)
+            rows = r[P * R_TILES * j : P * R_TILES * (j + 1), :]
+            nc.sync.dma_start(residual[j][:], rows.rearrange("(i p) m -> p i m", p=P))
+
+        load_halves(0, 2 * EARLY_GROUPS)
+        for quad in range(4):
+            nc.sync.dma_start(
+                key_scales[32 * quad : 32 * quad + 4 * K_PASSES, :].bitcast(I32),
+                tab_scales[:, 4 * quad : 4 * quad + 4, :].bitcast(I32),
+            )
+        for i, vec in enumerate((b, g)):
+            nc.sync.dma_start(
+                bg_rows[4 * i : 4 * i + 4, :].rearrange("t (q r) -> t q r", r=8),
+                vec.rearrange("(q t r) -> t q r", t=4, r=8),
+            )
+        for a in range(K_PASSES):
+            keys[a] = keep.tile([P, T], I32, name="keys%d" % a)
+            nc.sync.dma_start(keys[a][:], tab_words[a].rearrange("p n t -> p (n t)").bitcast(I32))
+            tokens[a] = placed("tokens%d" % a, [P, 4, M], F32, TOKEN_SLOT + a)
+            nc.sync.dma_start(tokens[a][:], x[PASS * a : PASS * (a + 1), :].rearrange("(p t) m -> p t m", t=4))
+        load_halves(2 * EARLY_GROUPS, 2 * EARLY_GROUPS + 2)
+        for quad in range(4):
+            nc.sync.dma_start(
+                dense_scales[32 * quad : 32 * quad + 4, :, :].bitcast(I32),
+                w4_scales[:, 4 * quad : 4 * quad + 4, :].rearrange("a s n -> s a n").bitcast(I32),
+            )
+        nc.sync.dma_start(dense[:].bitcast(I32), w4_words.rearrange("a p n -> p a n").bitcast(I32))
+        load_halves(2 * EARLY_GROUPS + 2, 2 * EARLY_GROUPS + 4)
+        load_residual(0)
+        load_halves(2 * EARLY_GROUPS + 4, 2 * GROUPS)
+        load_residual(1)
 
         def quantise(src, name):
             width = src.shape[1] // 4
-            if name + "_codes" in PLACE:
-                codes = placed(name + "_codes", [P, width], U32)
-            else:
-                codes = keep.tile([P, width], U32, name=name + "_codes", align_bytes=64)
+            codes = keep.tile([P, width], U32, name=name + "_codes", align_bytes=64)
             scales = keep.tile([P, width], U8, name=name + "_scales", align_bytes=64)
             nc.vector.quantize_mx(out=codes[:].bitcast(FP8X4), scales=scales[:], in_=src)
             return codes, scales
 
-        def woven_tile(name):
-            if name in PLACE:
-                return placed(name, [P, 4 * M], BF16)
-            return ring.tile([P, 4 * M], BF16, name="woven", tag="woven", bufs=3, align_bytes=64)
+        def woven_tile():
+            return ring.tile([P, 4 * M], BF16, name="woven", tag="woven", bufs=K_PASSES, align_bytes=64)
 
-        def step(what, i):
-            if what == "b":
-                bank = psum.tile([P, SP, P], F32, name="turned", tag="turned", bufs=3)
-                for a in range(SP):
-                    nc.tensor.transpose(bank[:, a, :], bg_rows[:, P * a : P * (a + 1)], ident[:])
-                nc.scalar.copy(bg[:], bank[:, :, 0:8])
-            elif what == "s":
-                listed_scales = keep.tile([P, S], U8, name="listed_scales", align_bytes=64)
-                nc.vector.tensor_copy(listed_scales[:], key_scales[:].indirect(offsets[:]))
-                nc.vector.tensor_copy(
-                    picked_scales[:].bitcast(I32).rearrange("p (t q w) -> p t q w", t=4, w=2),
-                    listed_scales[:].bitcast(I32).rearrange("p (q t w) -> p t q w", t=4, w=2),
-                )
-            elif what == "x":
-                woven = woven_tile("xw%d" % i)
-                dst = woven[:].rearrange("p (c i t) -> p c t i", i=4, t=4)
-                src = x_raw[i][:].rearrange("p t (c i) -> p c t i", i=4)
-                if X_ON[i] == "S":
-                    nc.scalar.copy(dst, src)
-                else:
+        def in_list_layout(tile):
+            return tile[:].rearrange("p (t q r) -> p q t r", t=4, r=8)
+
+        def gather_group(group):
+            pairs = placed("pairs%d" % group, [P, 2 * T], BF16, 0 if group % 2 else SPARE_SLOT)
+            for side in range(2):
+                dst = pairs[:, T * side : T * (side + 1)].rearrange("p (c e) -> p c e", e=2)
+                src = halves[2 * group + side][:].rearrange("p e c -> p c e")
+                if on_vector(2 * group + side):
                     nc.vector.tensor_copy(dst, src)
-                x_q[i] = quantise(woven[:], "x%d" % i)
-            elif what == "k":
-                picked[i] = keep.tile([P, S], U32, name="picked%d" % i, align_bytes=64)
-                nc.vector.tensor_copy(picked[i][:].rearrange("p (t q r) -> p q t r", t=4, r=8), keys[i][:].bitcast(U32).indirect(offsets[:]))
-            elif what == "c" or what == "C":
-                pair, half = divmod(i, 2)
-                if pair not in words:
-                    words[pair] = placed("words%d" % pair, [P, 2 * T], BF16)
-                dst = words[pair][:, T * half : T * (half + 1)].rearrange("p (c e) -> p c e", e=2)
-                src = wd_raw[i][:].rearrange("p e c -> p c e")
-                if what == "c":
-                    nc.scalar.copy(dst, src)
                 else:
-                    nc.vector.tensor_copy(dst, src)
-            elif what == "g":
-                got = ring.tile([P, S], U32, name="got", tag="got", bufs=2)
-                nc.vector.tensor_copy(got[:].rearrange("p (t q r) -> p q t r", t=4, r=8), words[i][:].bitcast(U32).indirect(offsets[:]))
-                for a in range(SP):
-                    bank = psum.tile([P, 4, P], F32, name="turned", tag="turned", bufs=3)
-                    for t in range(4):
-                        nc.tensor.transpose(bank[:, t, :], got[:, 256 * t + P * a : 256 * t + P * (a + 1)].bitcast(F32), ident[:])
-                    wb = placed("wb%d_%d" % (i, a), [P, 1024], BF16)
-                    nc.scalar.copy(
-                        wb[:].rearrange("p (c i t) -> p c t i", i=4, t=4),
-                        bank[:].rearrange("p t n -> p (t n)").bitcast(BF16).rearrange("p (t c i) -> p c t i", t=4, i=4),
-                    )
-                    turned[2 * i + a] = wb
-            elif what == "q":
-                pair, a = divmod(i, 2)
-                codes, scales = quantise(turned[i][:], "w%d" % i)
-                for h in range(2):
-                    wq[(2 * pair + h, a)] = (codes[:, P * h : P * (h + 1)], scales[:, P * h : P * (h + 1)])
-            elif what == "h":
-                acts[i] = placed("act%d" % i, [P, 4, M], F32)
+                    nc.scalar.copy(dst, src)
+            got = ring.tile([P, S], U32, name="got", tag="got")
+            nc.vector.tensor_copy(in_list_layout(got), pairs[:].bitcast(U32).indirect(offsets[:]))
+            for a in range(S_PASSES):
+                bank = psum.tile([P, 4, P], F32, name="turn", tag="turn", bufs=TURN_BANKS)
                 for t in range(4):
-                    bank = psum.tile([P, M], F32, name="acc", tag="acc", bufs=5)
-                    cols = slice(256 * t + P * i, 256 * t + P * (i + 1))
-                    for k in range(KP):
-                        nc.tensor.matmul_mx(
-                            out=bank[:],
-                            lhsT=picked[k][:, cols].bitcast(FP8X4),
-                            lhsT_scale=picked_scales[4 * k : P, cols],
-                            rhs=x_q[k][0][:].bitcast(FP8X4),
-                            rhs_scale=x_q[k][1][:],
-                            start=(k == 0),
-                            stop=(k == KP - 1),
-                        )
-                    nc.scalar.activation(acts[i][:, t, :], bank[:], ACT.Relu, bias=bg[:, i, t : t + 1])
-            elif what == "m":
-                wovens[i] = woven_tile("hw%d" % i)
-                nc.vector.tensor_tensor(
-                    wovens[i][:].rearrange("p (c i t) -> p c t i", i=4, t=4),
-                    acts[i][:].rearrange("p t (c i) -> p c t i", i=4),
-                    bg[:, i, 4:8].unsqueeze(1).unsqueeze(3).to_broadcast([P, M // 4, 4, 4]),
-                    ALU.mult,
+                    first = 256 * t + P * a
+                    nc.tensor.transpose(bank[:, t, :], got[:, first : first + P].bitcast(F32), ident[:])
+                flat = placed("turned%d_%d" % (group, a), [P, 4 * GROUP], BF16, turned_slot(group), 8 * GROUP * a)
+                nc.scalar.copy(
+                    flat[:].rearrange("p (c i t) -> p c t i", i=4, t=4),
+                    bank[:].rearrange("p t n -> p (t n)").bitcast(BF16).rearrange("p (t c i) -> p c t i", t=4, i=4),
                 )
-            elif what == "n":
-                h_q[i] = quantise(wovens[i][:], "h%d" % i)
-            elif what == "y":
-                bank = psum.tile([P, M], F32, name="acc", tag="acc", bufs=5)
-                for k in range(KP):
+                turned[group, a] = flat
+
+        def quantise_group(group):
+            for a in range(S_PASSES):
+                values_q[group, a] = quantise(turned[group, a][:], "values%d_%d" % (group, a))
+
+        def score_pass(a):
+            active = placed("active%d" % a, [P, 4, M], F32, 1 + a)
+            for t in range(4):
+                bank = psum.tile([P, M], F32, name="sum", tag="sum", bufs=SUM_BANKS)
+                cols = slice(256 * t + P * a, 256 * t + P * (a + 1))
+                for k in range(K_PASSES):
+                    nc.tensor.matmul_mx(
+                        out=bank[:],
+                        lhsT=picked[k][:, cols].bitcast(FP8X4),
+                        lhsT_scale=picked_scales[4 * k : P, cols],
+                        rhs=x_q[k][0][:].bitcast(FP8X4),
+                        rhs_scale=x_q[k][1][:],
+                        start=(k == 0),
+                        stop=(k == K_PASSES - 1),
+                    )
+                nc.scalar.activation(active[:, t, :], bank[:], ACT.Relu, bias=bg[:, a, t : t + 1])
+            woven_h[a] = woven_tile()
+            nc.vector.tensor_tensor(
+                woven_h[a][:].rearrange("p (c i t) -> p c t i", i=4, t=4),
+                active[:].rearrange("p t (c i) -> p c t i", i=4),
+                bg[:, a, 4:8].unsqueeze(1).unsqueeze(3).to_broadcast([P, M // 4, 4, 4]),
+                ALU.mult,
+            )
+
+        def output_group(group):
+            for side in range(2):
+                i = 2 * group + side
+                bank = psum.tile([P, M], F32, name="sum", tag="sum", bufs=SUM_BANKS)
+                for k in range(K_PASSES):
                     nc.tensor.matmul_mx(
                         out=bank[:],
                         lhsT=dense[:, k, 2 * P * i : 2 * P * (i + 1)].bitcast(FP4X4),
@@ -194,28 +192,61 @@ def tile_list_paged_memory_layer_kernel(tc, tab_words, tab_scales, offs, x, b, g
                         start=(k == 0),
                         stop=False,
                     )
-                for a in range(SP):
+                for a in range(S_PASSES):
+                    codes, scales = values_q[group, a]
                     nc.tensor.matmul_mx(
                         out=bank[:],
-                        lhsT=wq[(i, a)][0].bitcast(FP8X4),
-                        lhsT_scale=wq[(i, a)][1],
+                        lhsT=codes[:, P * side : P * (side + 1)].bitcast(FP8X4),
+                        lhsT_scale=scales[:, P * side : P * (side + 1)],
                         rhs=h_q[a][0][:].bitcast(FP8X4),
                         rhs_scale=h_q[a][1][:],
                         start=False,
-                        stop=(a == SP - 1),
+                        stop=(a == S_PASSES - 1),
                     )
-                banks[i] = bank
-            else:
-                mine = res[i // 4][:, i % 4, :]
-                results[i] = placed("out%d" % i, [P, M], F32)[:] if "out%d" % i in PLACE else mine
-                nc.vector.tensor_tensor(results[i], banks[i][:], mine, ALU.add)
+                results[i] = residual[i // R_TILES][:, i % R_TILES, :]
+                nc.vector.tensor_tensor(results[i], bank[:], results[i], ALU.add)
 
-        for what, i in LOADS:
-            if (what, i) != ("r", 2):
-                load(what, i)
-        for what, i in WORK:
-            if what == "y" and i == 0:
-                load("r", 2)
-            step(what, i)
+        bg_bank = psum.tile([P, S_PASSES, P], F32, name="turn", tag="turn", bufs=TURN_BANKS)
+        for a in range(S_PASSES):
+            nc.tensor.transpose(bg_bank[:, a, :], bg_rows[:, P * a : P * (a + 1)], ident[:])
+        nc.scalar.copy(bg[:], bg_bank[:, :, 0:8])
+
+        listed_scales = keep.tile([P, S], U8, name="listed_scales", align_bytes=64)
+        nc.vector.tensor_copy(listed_scales[:], key_scales[:].indirect(offsets[:]))
+        nc.vector.tensor_copy(
+            picked_scales[:].bitcast(I32).rearrange("p (t q w) -> p t q w", t=4, w=2),
+            listed_scales[:].bitcast(I32).rearrange("p (q t w) -> p t q w", t=4, w=2),
+        )
+
+        for group in range(EARLY_GROUPS):
+            gather_group(group)
+        for a in range(K_PASSES):
+            woven_x = woven_tile()
+            nc.scalar.copy(
+                woven_x[:].rearrange("p (c i t) -> p c t i", i=4, t=4),
+                tokens[a][:].rearrange("p t (c i) -> p c t i", i=4),
+            )
+            x_q[a] = quantise(woven_x[:], "x%d" % a)
+            picked[a] = keep.tile([P, S], U32, name="picked%d" % a, align_bytes=64)
+            nc.vector.tensor_copy(in_list_layout(picked[a]), keys[a][:].bitcast(U32).indirect(offsets[:]))
+            if a < EARLY_GROUPS:
+                quantise_group(a)
+
+        gather_group(EARLY_GROUPS)
+        for a in range(S_PASSES):
+            score_pass(a)
+        for a in range(S_PASSES):
+            h_q[a] = quantise(woven_h[a][:], "h%d" % a)
+        load_residual(2)
+        output_group(0)
+
+        for group in range(EARLY_GROUPS + 1, GROUPS):
+            gather_group(group)
+            quantise_group(group - 1)
+            output_group(group - 2)
+        output_group(GROUPS - 2)
+        quantise_group(GROUPS - 1)
+        output_group(GROUPS - 1)
+
         for i in range(N // P):
             nc.sync.dma_start(out[P * i : P * (i + 1), :], results[i])

@@ -21,29 +21,19 @@ P = 128
 PASS = 4 * P
 K_PASSES = K // PASS
 S_PASSES = S // PASS
-GROUP = 2 * P
-GROUPS = N // GROUP
-R_TILES = 4
-EARLY_GROUPS = 2
-VECTOR_EVERY = 3
 SUM_BANKS, TURN_BANKS = 6, 2
+UNIT_TILES = (2, 1, 1, 2, 1, 2, 1, 2)
+FIRST_TILE = tuple(sum(UNIT_TILES[:u]) for u in range(len(UNIT_TILES)))
 
 SLOT = 8192
-SPARE_SLOT = 2 * GROUPS
-TOKEN_SLOT = SPARE_SLOT + 1
-
-
-def on_vector(half):
-    return half % (2 * VECTOR_EVERY) == 2 * VECTOR_EVERY - 1
-
-
-def turned_slot(group):
-    if group == EARLY_GROUPS - 1:
-        return TOKEN_SLOT
-    if group == GROUPS - 1:
-        return 2 * EARLY_GROUPS
-    last = 2 * group + 3
-    return last - 1 if on_vector(last) else last
+TOKEN_SLOT = N // P
+KEY_SLOT = TOKEN_SLOT + K_PASSES
+RESIDUAL_SLOT = KEY_SLOT + K_PASSES
+PICKED_SLOT = RESIDUAL_SLOT + 3
+HALF = SLOT // 2
+PAIRS_AT = {3: (PICKED_SLOT, HALF), 5: (5, 0), 7: (8, 0)}
+GOT_AT = {1: (PICKED_SLOT + 1, HALF), 0: (KEY_SLOT, 0), 2: (KEY_SLOT + 2, 0), 3: (KEY_SLOT, HALF), 4: (KEY_SLOT + 1, 0), 5: (KEY_SLOT, 0), 6: (KEY_SLOT + 1, HALF), 7: (9, 0)}
+TURNED_AT = {1: (TOKEN_SLOT, 0), 0: (TOKEN_SLOT + 2, 0), 2: (4, 0), 3: (7, 0), 4: (3, 0), 5: (10, 0), 6: (3, 2048), 7: (0, 0)}
 
 
 def tile_list_paged_memory_layer_kernel(tc, tab_words, tab_scales, offs, x, b, g, wdT, w4_words, w4_scales, r, out):
@@ -62,154 +52,253 @@ def tile_list_paged_memory_layer_kernel(tc, tab_words, tab_scales, offs, x, b, g
 
         key_scales = keep.tile([P, T], U8, name="key_scales", align_bytes=64)
         nc.gpsimd.memset(key_scales[:].bitcast(I32), 0)
-        bg_rows = keep.tile([P, S_PASSES * P], F32, name="bg_rows")
-        nc.gpsimd.memset(bg_rows[:], 0.0)
         dense_scales = keep.tile([P, K_PASSES, N], U8, name="dense_scales", align_bytes=64)
         nc.vector.memset(dense_scales[:].rearrange("p a n -> p (a n)").bitcast(I32), 0)
+        bg_rows = keep.tile([P, PASS], F32, name="bg_rows")
+        nc.vector.memset(bg_rows[:], 0.0)
         ident = keep.tile([P, P], F32, name="ident")
         make_identity(nc, ident[:])
+        ident16 = keep.tile([P, P], BF16, name="ident16")
+        make_identity(nc, ident16[:])
         dense = keep.tile([P, K_PASSES, 2 * N], U8, name="dense", align_bytes=64)
-        bg = keep.tile([P, S_PASSES, 8], F32, name="bg")
+        bg = keep.tile([P, 4, 2 * S_PASSES], F32, name="bg")
+        bg_raw = keep.tile([2 * S_PASSES, PASS], F32, name="bg_raw")
         picked_scales = keep.tile([P, S], U8, name="picked_scales", align_bytes=64)
-        tokens, keys, halves, residual = {}, {}, {}, {}
-        x_q, picked, turned, values_q, woven_h, h_q, results = {}, {}, {}, {}, {}, {}, {}
+        tokens, keys, values, residual = {}, {}, {}, {}
+        x_q, picked, pairs, got, turned, values_q, woven_h, h_q, sums, banks = {}, {}, {}, {}, {}, {}, {}, {}, {}, {}
 
-        def load_halves(first, stop):
-            for half in range(first, stop):
-                group, side = divmod(half, 2)
-                halves[half] = placed("half%d" % half, [P, 2, T // 2], F32, half)
-                rows = wdT[GROUP * group : GROUP * (group + 1), T // 2 * side : T // 2 * (side + 1)]
-                nc.sync.dma_start(halves[half][:], rows.rearrange("(p e) c -> p e c", e=2))
+        def load_values(unit):
+            tiles, first = UNIT_TILES[unit], FIRST_TILE[unit]
+            values[unit] = placed("values%d" % unit, [P, tiles, T], F32, first)
+            rows = wdT[P * first : P * (first + tiles), :]
+            nc.sync.dma_start(values[unit][:], rows.rearrange("(p e) c -> p e c", e=tiles))
 
-        def load_residual(j):
-            residual[j] = placed("residual%d" % j, [P, R_TILES, M], F32, TOKEN_SLOT + (j + 1) % K_PASSES)
-            rows = r[P * R_TILES * j : P * R_TILES * (j + 1), :]
-            nc.sync.dma_start(residual[j][:], rows.rearrange("(i p) m -> p i m", p=P))
-
-        load_halves(0, 2 * EARLY_GROUPS)
-        for quad in range(4):
-            nc.sync.dma_start(
-                key_scales[32 * quad : 32 * quad + 4 * K_PASSES, :].bitcast(I32),
-                tab_scales[:, 4 * quad : 4 * quad + 4, :].bitcast(I32),
-            )
-        for i, vec in enumerate((b, g)):
-            nc.sync.dma_start(
-                bg_rows[4 * i : 4 * i + 4, :].rearrange("t (q r) -> t q r", r=8),
-                vec.rearrange("(q t r) -> t q r", t=4, r=8),
-            )
-        for a in range(K_PASSES):
-            keys[a] = keep.tile([P, T], I32, name="keys%d" % a)
-            nc.sync.dma_start(keys[a][:], tab_words[a].rearrange("p n t -> p (n t)").bitcast(I32))
+        def load_tokens(a):
             tokens[a] = placed("tokens%d" % a, [P, 4, M], F32, TOKEN_SLOT + a)
             nc.sync.dma_start(tokens[a][:], x[PASS * a : PASS * (a + 1), :].rearrange("(p t) m -> p t m", t=4))
-        load_halves(2 * EARLY_GROUPS, 2 * EARLY_GROUPS + 2)
-        for quad in range(4):
-            nc.sync.dma_start(
-                dense_scales[32 * quad : 32 * quad + 4, :, :].bitcast(I32),
-                w4_scales[:, 4 * quad : 4 * quad + 4, :].rearrange("a s n -> s a n").bitcast(I32),
-            )
-        nc.sync.dma_start(dense[:].bitcast(I32), w4_words.rearrange("a p n -> p a n").bitcast(I32))
-        load_halves(2 * EARLY_GROUPS + 2, 2 * EARLY_GROUPS + 4)
-        load_residual(0)
-        load_halves(2 * EARLY_GROUPS + 4, 2 * GROUPS)
-        load_residual(1)
 
-        def quantise(src, name):
+        def load_keys(a):
+            keys[a] = placed("keys%d" % a, [P, T], I32, KEY_SLOT + a)
+            nc.sync.dma_start(keys[a][:], tab_words[a].rearrange("p n t -> p (n t)").bitcast(I32))
+
+        def load_residual(first, stop):
+            tile = placed("residual%d" % first, [P, stop - first, M], F32, RESIDUAL_SLOT, 4 * M * first)
+            nc.sync.dma_start(tile[:], r[P * first : P * stop, :].rearrange("(i p) m -> p i m", p=P))
+            for i in range(first, stop):
+                residual[i] = tile[:, i - first, :]
+
+        def load_key_scales():
+            for quad in range(4):
+                nc.sync.dma_start(
+                    key_scales[32 * quad : 32 * quad + 4 * K_PASSES, :].bitcast(I32),
+                    tab_scales[:, 4 * quad : 4 * quad + 4, :].bitcast(I32),
+                )
+
+        def load_dense_scales():
+            for s in range(4):
+                nc.gpsimd.dma_start(
+                    dense_scales[s:P:32, :, :].bitcast(I32),
+                    w4_scales[:, s:16:4, :].rearrange("a q n -> q a n").bitcast(I32),
+                )
+
+        for i, vec in enumerate((b, g)):
+            nc.sync.dma_start(bg_raw[S_PASSES * i : S_PASSES * (i + 1), :], vec.rearrange("(a j) -> a j", a=S_PASSES))
+        load_tokens(0)
+        load_keys(0)
+        load_values(1)
+        load_key_scales()
+        load_dense_scales()
+        load_values(0)
+        load_keys(1)
+        load_tokens(1)
+        load_tokens(2)
+        load_keys(2)
+        load_values(2)
+        load_values(3)
+        nc.sync.dma_start(dense[:].bitcast(I32), w4_words.rearrange("a p n -> p a n").bitcast(I32))
+        load_residual(0, 2)
+        load_values(5)
+        load_values(4)
+        load_values(7)
+        load_residual(2, 7)
+        load_values(6)
+        load_residual(7, 10)
+        load_residual(10, 12)
+
+        def quantise(src, name, slot=None, at=0):
             width = src.shape[1] // 4
-            codes = keep.tile([P, width], U32, name=name + "_codes", align_bytes=64)
-            scales = keep.tile([P, width], U8, name=name + "_scales", align_bytes=64)
+            if slot is None:
+                codes = keep.tile([P, width], U32, name=name + "_codes", align_bytes=64)
+                scales = keep.tile([P, width], U8, name=name + "_scales", align_bytes=64)
+            else:
+                codes = placed(name + "_codes", [P, width], U32, slot, at)
+                scales = placed(name + "_scales", [P, width], U8, slot, at + 4 * width)
             nc.vector.quantize_mx(out=codes[:].bitcast(FP8X4), scales=scales[:], in_=src)
             return codes, scales
 
         def woven_tile():
-            return ring.tile([P, 4 * M], BF16, name="woven", tag="woven", bufs=K_PASSES, align_bytes=64)
+            return ring.tile([P, 4 * M], BF16, name="woven", tag="woven", bufs=2, align_bytes=64)
 
         def in_list_layout(tile):
             return tile[:].rearrange("p (t q r) -> p q t r", t=4, r=8)
 
-        def gather_group(group):
-            pairs = placed("pairs%d" % group, [P, 2 * T], BF16, 0 if group % 2 else SPARE_SLOT)
-            for side in range(2):
-                dst = pairs[:, T * side : T * (side + 1)].rearrange("p (c e) -> p c e", e=2)
-                src = halves[2 * group + side][:].rearrange("p e c -> p c e")
-                if on_vector(2 * group + side):
-                    nc.vector.tensor_copy(dst, src)
-                else:
-                    nc.scalar.copy(dst, src)
-            got = ring.tile([P, S], U32, name="got", tag="got")
-            nc.vector.tensor_copy(in_list_layout(got), pairs[:].bitcast(U32).indirect(offsets[:]))
-            for a in range(S_PASSES):
-                bank = psum.tile([P, 4, P], F32, name="turn", tag="turn", bufs=TURN_BANKS)
-                for t in range(4):
-                    first = 256 * t + P * a
-                    nc.tensor.transpose(bank[:, t, :], got[:, first : first + P].bitcast(F32), ident[:])
-                flat = placed("turned%d_%d" % (group, a), [P, 4 * GROUP], BF16, turned_slot(group), 8 * GROUP * a)
-                nc.scalar.copy(
-                    flat[:].rearrange("p (c i t) -> p c t i", i=4, t=4),
-                    bank[:].rearrange("p t n -> p (t n)").bitcast(BF16).rearrange("p (t c i) -> p c t i", t=4, i=4),
-                )
-                turned[group, a] = flat
+        def gather_words(window, parts):
+            if len(parts) == 1:
+                dst = parts[0]
+                nc.vector.tensor_copy(in_list_layout(dst), window.indirect(offsets[:]))
+                return [[dst[:, 256 * t + P * a : 256 * t + P * (a + 1)] for t in range(4)] for a in range(S_PASSES)]
+            for a, dst in enumerate(parts):
+                nc.vector.tensor_copy(in_list_layout(dst), window.indirect(offsets[:, 32 * a : 32 * (a + 1)]))
+            return [[dst[:, P * t : P * (t + 1)] for t in range(4)] for dst in parts]
 
-        def quantise_group(group):
+        def round_pairs(unit):
+            if unit == 0:
+                pairs[unit] = keep.tile([P, 2 * T], BF16, name="pairs0", align_bytes=64)
+            else:
+                pairs[unit] = placed("pairs%d" % unit, [P, 2 * T], BF16, *PAIRS_AT[unit])
+            nc.scalar.copy(pairs[unit][:].rearrange("p (c e) -> p c e", e=2), values[unit][:].rearrange("p e c -> p c e"))
+
+        def gather_values(unit):
+            if UNIT_TILES[unit] == 1:
+                dst = placed("got%d" % unit, [P, S], BF16, *GOT_AT[unit])
+                nc.vector.tensor_copy(in_list_layout(dst), values[unit][:, 0, :].indirect(offsets[:]))
+                got[unit] = [[dst[:, 256 * t + P * a : 256 * t + P * (a + 1)] for t in range(4)] for a in range(S_PASSES)]
+                return
+            if unit == 7:
+                parts = [placed("got%d_%d" % (unit, a), [P, PASS], U32, GOT_AT[unit][0], 4 * PASS * a) for a in range(S_PASSES)]
+            else:
+                parts = [placed("got%d" % unit, [P, S], U32, *GOT_AT[unit])]
+            got[unit] = gather_words(pairs[unit][:].bitcast(U32), parts)
+
+        def transpose_values(unit):
+            tag, bufs = ("sum", SUM_BANKS) if unit == 2 else ("turn", TURN_BANKS)
+            if UNIT_TILES[unit] == 1:
+                bank = psum.tile([P, S_PASSES, 4, P], BF16, name=tag, tag=tag, bufs=bufs)
+                for a in range(S_PASSES):
+                    for t in range(4):
+                        nc.tensor.transpose(bank[:, a, t, :], got[unit][a][t], ident16[:])
+                banks[unit] = [bank[:].rearrange("p a t n -> p (a t n)")]
+                return
+            banks[unit] = []
             for a in range(S_PASSES):
-                values_q[group, a] = quantise(turned[group, a][:], "values%d_%d" % (group, a))
+                bank = psum.tile([P, 4, P], F32, name=tag, tag=tag, bufs=bufs)
+                for t in range(4):
+                    nc.tensor.transpose(bank[:, t, :], got[unit][a][t].bitcast(F32), ident[:])
+                banks[unit].append(bank[:].rearrange("p t n -> p (t n)").bitcast(BF16))
+
+        def weave_values(unit):
+            slot, at = TURNED_AT[unit]
+            turned[unit] = []
+            for n, bank in enumerate(banks[unit]):
+                flat = placed("turned%d_%d" % (unit, n), [P, S], BF16, slot, at + 2 * S * n)
+                if UNIT_TILES[unit] == 1:
+                    nc.scalar.copy(
+                        flat[:].rearrange("p (a n t) -> p a n t", a=S_PASSES, t=4),
+                        bank.rearrange("p (a t n) -> p a n t", a=S_PASSES, t=4),
+                    )
+                else:
+                    nc.scalar.copy(flat[:].rearrange("p (n t) -> p n t", t=4), bank.rearrange("p (t n) -> p n t", t=4))
+                turned[unit].append(flat)
+
+        def quantise_values(unit):
+            for n, flat in enumerate(turned[unit]):
+                where = (9, 0) if (unit, n) == (5, 0) else (FIRST_TILE[unit], HALF + 5 * 2 * P * n)
+                codes, scales = quantise(flat[:], "values%d_%d" % (unit, n), *where)
+                for half in range(2):
+                    cols = slice(P * half, P * (half + 1))
+                    key = (FIRST_TILE[unit] + half, n) if UNIT_TILES[unit] == 2 else (FIRST_TILE[unit], half)
+                    values_q[key] = codes[:, cols], scales[:, cols]
+
+        def weave_tokens(a):
+            woven_x = woven_tile()
+            nc.scalar.copy(
+                woven_x[:].rearrange("p (c i t) -> p c t i", i=4, t=4),
+                tokens[a][:].rearrange("p t (c i) -> p c t i", i=4),
+            )
+            x_q[a] = quantise(woven_x[:], "x%d" % a)
+
+        def gather_keys(k):
+            if k + 1 < K_PASSES:
+                parts = [placed("picked%d" % k, [P, S], U32, PICKED_SLOT, HALF * k)]
+            else:
+                parts = [placed("picked%d_%d" % (k, a), [P, PASS], U32, PICKED_SLOT + 1, 4 * PASS * a) for a in range(S_PASSES)]
+            picked[k] = gather_words(keys[k][:].bitcast(U32), parts)
 
         def score_pass(a):
-            active = placed("active%d" % a, [P, 4, M], F32, 1 + a)
+            active = placed("active%d" % a, [P, 4, M], F32, TOKEN_SLOT + 1 + a)
             for t in range(4):
                 bank = psum.tile([P, M], F32, name="sum", tag="sum", bufs=SUM_BANKS)
                 cols = slice(256 * t + P * a, 256 * t + P * (a + 1))
                 for k in range(K_PASSES):
                     nc.tensor.matmul_mx(
                         out=bank[:],
-                        lhsT=picked[k][:, cols].bitcast(FP8X4),
+                        lhsT=picked[k][a][t].bitcast(FP8X4),
                         lhsT_scale=picked_scales[4 * k : P, cols],
                         rhs=x_q[k][0][:].bitcast(FP8X4),
                         rhs_scale=x_q[k][1][:],
                         start=(k == 0),
                         stop=(k == K_PASSES - 1),
                     )
-                nc.scalar.activation(active[:, t, :], bank[:], ACT.Relu, bias=bg[:, a, t : t + 1])
-            woven_h[a] = woven_tile()
+                nc.scalar.activation(active[:, t, :], bank[:], ACT.Relu, bias=bg[:, t, a : a + 1])
+            woven_h[a] = placed("woven_h%d" % a, [P, 4 * M], BF16, TOKEN_SLOT, HALF * (1 - a))
             nc.vector.tensor_tensor(
                 woven_h[a][:].rearrange("p (c i t) -> p c t i", i=4, t=4),
                 active[:].rearrange("p t (c i) -> p c t i", i=4),
-                bg[:, a, 4:8].unsqueeze(1).unsqueeze(3).to_broadcast([P, M // 4, 4, 4]),
+                bg[:, :, S_PASSES + a : S_PASSES + a + 1].unsqueeze(1).to_broadcast([P, M // 4, 4, 4]),
                 ALU.mult,
             )
+            h_q[a] = quantise(woven_h[a][:], "h%d" % a, TOKEN_SLOT + 1 + a)
 
-        def output_group(group):
-            for side in range(2):
-                i = 2 * group + side
-                bank = psum.tile([P, M], F32, name="sum", tag="sum", bufs=SUM_BANKS)
-                for k in range(K_PASSES):
+        def tiles_of(unit):
+            return range(FIRST_TILE[unit], FIRST_TILE[unit] + UNIT_TILES[unit])
+
+        def dense_tile(i):
+            sums[i] = psum.tile([P, M], F32, name="sum", tag="sum", bufs=SUM_BANKS)
+            for k in range(K_PASSES):
+                nc.tensor.matmul_mx(
+                    out=sums[i][:],
+                    lhsT=dense[:, k, 2 * P * i : 2 * P * (i + 1)].bitcast(FP4X4),
+                    lhsT_scale=dense_scales[:, k, P * i : P * (i + 1)],
+                    rhs=x_q[k][0][:].bitcast(FP8X4),
+                    rhs_scale=x_q[k][1][:],
+                    start=(k == 0),
+                    stop=False,
+                )
+
+        def dense_passes(unit):
+            for i in tiles_of(unit):
+                dense_tile(i)
+
+        def mix_passes(unit):
+            for a in range(S_PASSES):
+                for i in tiles_of(unit):
+                    codes, scales = values_q[i, a]
                     nc.tensor.matmul_mx(
-                        out=bank[:],
-                        lhsT=dense[:, k, 2 * P * i : 2 * P * (i + 1)].bitcast(FP4X4),
-                        lhsT_scale=dense_scales[:, k, P * i : P * (i + 1)],
-                        rhs=x_q[k][0][:].bitcast(FP8X4),
-                        rhs_scale=x_q[k][1][:],
-                        start=(k == 0),
-                        stop=False,
-                    )
-                for a in range(S_PASSES):
-                    codes, scales = values_q[group, a]
-                    nc.tensor.matmul_mx(
-                        out=bank[:],
-                        lhsT=codes[:, P * side : P * (side + 1)].bitcast(FP8X4),
-                        lhsT_scale=scales[:, P * side : P * (side + 1)],
+                        out=sums[i][:],
+                        lhsT=codes.bitcast(FP8X4),
+                        lhsT_scale=scales,
                         rhs=h_q[a][0][:].bitcast(FP8X4),
                         rhs_scale=h_q[a][1][:],
                         start=False,
                         stop=(a == S_PASSES - 1),
                     )
-                results[i] = residual[i // R_TILES][:, i % R_TILES, :]
-                nc.vector.tensor_tensor(results[i], bank[:], results[i], ALU.add)
 
-        bg_bank = psum.tile([P, S_PASSES, P], F32, name="turn", tag="turn", bufs=TURN_BANKS)
-        for a in range(S_PASSES):
-            nc.tensor.transpose(bg_bank[:, a, :], bg_rows[:, P * a : P * (a + 1)], ident[:])
-        nc.scalar.copy(bg[:], bg_bank[:, :, 0:8])
+        def add_residual(unit):
+            for i in tiles_of(unit):
+                nc.vector.tensor_tensor(residual[i], sums[i][:], residual[i], ALU.add)
+
+        def finish_values(unit):
+            weave_values(unit)
+            quantise_values(unit)
+
+        nc.scalar.copy(
+            bg_rows[0 : 2 * S_PASSES, :].rearrange("p (t q r) -> p t q r", t=4, r=8),
+            bg_raw[:].rearrange("p (q t r) -> p t q r", t=4, r=8),
+        )
+        bg_bank = psum.tile([P, 4, P], F32, name="turn", tag="turn", bufs=TURN_BANKS)
+        for t in range(4):
+            nc.tensor.transpose(bg_bank[:, t, :], bg_rows[:, P * t : P * (t + 1)], ident[:])
+        nc.scalar.copy(bg[:], bg_bank[:, :, 0 : 2 * S_PASSES])
 
         listed_scales = keep.tile([P, S], U8, name="listed_scales", align_bytes=64)
         nc.vector.tensor_copy(listed_scales[:], key_scales[:].indirect(offsets[:]))
@@ -218,35 +307,66 @@ def tile_list_paged_memory_layer_kernel(tc, tab_words, tab_scales, offs, x, b, g
             listed_scales[:].bitcast(I32).rearrange("p (q t w) -> p t q w", t=4, w=2),
         )
 
-        for group in range(EARLY_GROUPS):
-            gather_group(group)
-        for a in range(K_PASSES):
-            woven_x = woven_tile()
-            nc.scalar.copy(
-                woven_x[:].rearrange("p (c i t) -> p c t i", i=4, t=4),
-                tokens[a][:].rearrange("p t (c i) -> p c t i", i=4),
-            )
-            x_q[a] = quantise(woven_x[:], "x%d" % a)
-            picked[a] = keep.tile([P, S], U32, name="picked%d" % a, align_bytes=64)
-            nc.vector.tensor_copy(in_list_layout(picked[a]), keys[a][:].bitcast(U32).indirect(offsets[:]))
-            if a < EARLY_GROUPS:
-                quantise_group(a)
-
-        gather_group(EARLY_GROUPS)
+        weave_tokens(0)
+        gather_keys(0)
+        gather_values(1)
+        transpose_values(1)
+        finish_values(1)
+        round_pairs(0)
+        gather_keys(1)
+        gather_values(0)
+        transpose_values(0)
+        weave_tokens(1)
+        weave_tokens(2)
+        weave_values(0)
+        gather_keys(2)
+        quantise_values(0)
+        gather_values(2)
         for a in range(S_PASSES):
             score_pass(a)
-        for a in range(S_PASSES):
-            h_q[a] = quantise(woven_h[a][:], "h%d" % a)
-        load_residual(2)
-        output_group(0)
-
-        for group in range(EARLY_GROUPS + 1, GROUPS):
-            gather_group(group)
-            quantise_group(group - 1)
-            output_group(group - 2)
-        output_group(GROUPS - 2)
-        quantise_group(GROUPS - 1)
-        output_group(GROUPS - 1)
+        round_pairs(3)
+        transpose_values(2)
+        weave_values(2)
+        gather_values(3)
+        quantise_values(2)
+        for unit in range(3):
+            dense_passes(unit)
+            mix_passes(unit)
+        transpose_values(3)
+        add_residual(0)
+        for i in range(4, 8):
+            dense_tile(i)
+        round_pairs(5)
+        gather_values(4)
+        gather_values(5)
+        weave_values(3)
+        transpose_values(4)
+        weave_values(4)
+        transpose_values(5)
+        for unit in range(3, 5):
+            quantise_values(unit)
+            mix_passes(unit)
+        round_pairs(7)
+        for unit in range(1, 4):
+            add_residual(unit)
+        for i in range(8, 12):
+            dense_tile(i)
+        add_residual(4)
+        gather_values(6)
+        gather_values(7)
+        weave_values(5)
+        transpose_values(6)
+        weave_values(6)
+        transpose_values(7)
+        for unit in range(5, 7):
+            quantise_values(unit)
+            mix_passes(unit)
+        weave_values(7)
+        add_residual(5)
+        quantise_values(7)
+        add_residual(6)
+        mix_passes(7)
+        add_residual(7)
 
         for i in range(N // P):
-            nc.sync.dma_start(out[P * i : P * (i + 1), :], results[i])
+            nc.sync.dma_start(out[P * i : P * (i + 1), :], residual[i])

@@ -22,7 +22,7 @@ PASS = 4 * P
 K_PASSES = K // PASS
 S_PASSES = S // PASS
 SUM_BANKS, TURN_BANKS = 6, 2
-UNIT_TILES = (2, 1, 1, 2, 1, 2, 1, 2)
+UNIT_TILES = (2, 2, 2, 2, 2, 1, 1)
 FIRST_TILE = tuple(sum(UNIT_TILES[:u]) for u in range(len(UNIT_TILES)))
 
 SLOT = 8192
@@ -31,9 +31,11 @@ KEY_SLOT = TOKEN_SLOT + K_PASSES
 RESIDUAL_SLOT = KEY_SLOT + K_PASSES
 PICKED_SLOT = RESIDUAL_SLOT + 3
 HALF = SLOT // 2
-PAIRS_AT = {3: (PICKED_SLOT, HALF), 5: (5, 0), 7: (8, 0)}
-GOT_AT = {1: (PICKED_SLOT + 1, HALF), 0: (KEY_SLOT, 0), 2: (KEY_SLOT + 2, 0), 3: (KEY_SLOT, HALF), 4: (KEY_SLOT + 1, 0), 5: (KEY_SLOT, 0), 6: (KEY_SLOT + 1, HALF), 7: (9, 0)}
-TURNED_AT = {1: (TOKEN_SLOT, 0), 0: (TOKEN_SLOT + 2, 0), 2: (4, 0), 3: (7, 0), 4: (3, 0), 5: (10, 0), 6: (3, 2048), 7: (0, 0)}
+PAIRS_AT = {1: (0, 0), 2: (PICKED_SLOT, HALF), 3: (5, 0), 4: (7, 0)}
+GOT_AT = {0: (PICKED_SLOT + 1, HALF), 1: (1, 0), 2: (KEY_SLOT, 0), 3: (KEY_SLOT, HALF), 4: (KEY_SLOT + 1, 0), 5: (KEY_SLOT + 1, HALF), 6: (KEY_SLOT + 2, 0)}
+TURNED_AT = {0: (2, 0), 1: (TOKEN_SLOT + 2, 0), 2: (6, 0), 3: (8, 0), 4: (0, 0), 5: (3, 0), 6: (3, 2048)}
+CODES_AT = {0: (1, HALF), 1: (2, HALF), 2: (4, HALF), 3: (6, HALF), 4: (8, HALF), 5: (10, HALF), 6: (11, HALF)}
+GPSIMD_COLUMNS = 0
 
 
 def tile_list_paged_memory_layer_kernel(tc, tab_words, tab_scales, offs, x, b, g, wdT, w4_words, w4_scales, r, out):
@@ -69,6 +71,14 @@ def tile_list_paged_memory_layer_kernel(tc, tab_words, tab_scales, offs, x, b, g
 
         def load_values(unit):
             tiles, first = UNIT_TILES[unit], FIRST_TILE[unit]
+            if unit == 0:
+                values[unit] = []
+                for side in range(2):
+                    half = placed("values0_%d" % side, [P, 2, T // 2], F32, side)
+                    rows = wdT[0 : 2 * P, T // 2 * side : T // 2 * (side + 1)]
+                    nc.sync.dma_start(half[:], rows.rearrange("(p e) c -> p e c", e=2))
+                    values[unit].append(half)
+                return
             values[unit] = placed("values%d" % unit, [P, tiles, T], F32, first)
             rows = wdT[P * first : P * (first + tiles), :]
             nc.sync.dma_start(values[unit][:], rows.rearrange("(p e) c -> p e c", e=tiles))
@@ -103,27 +113,26 @@ def tile_list_paged_memory_layer_kernel(tc, tab_words, tab_scales, offs, x, b, g
 
         for i, vec in enumerate((b, g)):
             nc.sync.dma_start(bg_raw[S_PASSES * i : S_PASSES * (i + 1), :], vec.rearrange("(a j) -> a j", a=S_PASSES))
-        load_tokens(0)
-        load_keys(0)
+        load_values(0)
         load_values(1)
         load_key_scales()
         load_dense_scales()
-        load_values(0)
+        load_keys(0)
+        load_tokens(0)
         load_keys(1)
         load_tokens(1)
         load_tokens(2)
         load_keys(2)
         load_values(2)
-        load_values(3)
         nc.sync.dma_start(dense[:].bitcast(I32), w4_words.rearrange("a p n -> p a n").bitcast(I32))
-        load_residual(0, 2)
-        load_values(5)
+        load_values(3)
+        load_residual(0, 4)
         load_values(4)
-        load_values(7)
-        load_residual(2, 7)
+        load_values(5)
+        load_residual(4, 6)
         load_values(6)
-        load_residual(7, 10)
-        load_residual(10, 12)
+        load_residual(6, 9)
+        load_residual(9, 12)
 
         def quantise(src, name, slot=None, at=0):
             width = src.shape[1] // 4
@@ -156,7 +165,16 @@ def tile_list_paged_memory_layer_kernel(tc, tab_words, tab_scales, offs, x, b, g
                 pairs[unit] = keep.tile([P, 2 * T], BF16, name="pairs0", align_bytes=64)
             else:
                 pairs[unit] = placed("pairs%d" % unit, [P, 2 * T], BF16, *PAIRS_AT[unit])
-            nc.scalar.copy(pairs[unit][:].rearrange("p (c e) -> p c e", e=2), values[unit][:].rearrange("p e c -> p c e"))
+            dst = pairs[unit][:].rearrange("p (c e) -> p c e", e=2)
+            if unit == 0:
+                for side, half in enumerate(values[unit]):
+                    nc.scalar.copy(dst[:, T // 2 * side : T // 2 * (side + 1), :], half[:].rearrange("p e c -> p c e"))
+                return
+            src = values[unit][:].rearrange("p e c -> p c e")
+            cut = GPSIMD_COLUMNS if unit >= 2 else 0
+            if cut:
+                nc.gpsimd.tensor_copy(dst[:, 0:cut, :], src[:, 0:cut, :])
+            nc.scalar.copy(dst[:, cut:T, :], src[:, cut:T, :])
 
         def gather_values(unit):
             if UNIT_TILES[unit] == 1:
@@ -164,14 +182,14 @@ def tile_list_paged_memory_layer_kernel(tc, tab_words, tab_scales, offs, x, b, g
                 nc.vector.tensor_copy(in_list_layout(dst), values[unit][:, 0, :].indirect(offsets[:]))
                 got[unit] = [[dst[:, 256 * t + P * a : 256 * t + P * (a + 1)] for t in range(4)] for a in range(S_PASSES)]
                 return
-            if unit == 7:
+            if unit == 4:
                 parts = [placed("got%d_%d" % (unit, a), [P, PASS], U32, GOT_AT[unit][0], 4 * PASS * a) for a in range(S_PASSES)]
             else:
                 parts = [placed("got%d" % unit, [P, S], U32, *GOT_AT[unit])]
             got[unit] = gather_words(pairs[unit][:].bitcast(U32), parts)
 
         def transpose_values(unit):
-            tag, bufs = ("sum", SUM_BANKS) if unit == 2 else ("turn", TURN_BANKS)
+            tag, bufs = "turn", TURN_BANKS
             if UNIT_TILES[unit] == 1:
                 bank = psum.tile([P, S_PASSES, 4, P], BF16, name=tag, tag=tag, bufs=bufs)
                 for a in range(S_PASSES):
@@ -202,8 +220,8 @@ def tile_list_paged_memory_layer_kernel(tc, tab_words, tab_scales, offs, x, b, g
 
         def quantise_values(unit):
             for n, flat in enumerate(turned[unit]):
-                where = (9, 0) if (unit, n) == (5, 0) else (FIRST_TILE[unit], HALF + 5 * 2 * P * n)
-                codes, scales = quantise(flat[:], "values%d_%d" % (unit, n), *where)
+                slot, at = CODES_AT[unit]
+                codes, scales = quantise(flat[:], "values%d_%d" % (unit, n), slot, at + 5 * 2 * P * n)
                 for half in range(2):
                     cols = slice(P * half, P * (half + 1))
                     key = (FIRST_TILE[unit] + half, n) if UNIT_TILES[unit] == 2 else (FIRST_TILE[unit], half)
@@ -307,66 +325,60 @@ def tile_list_paged_memory_layer_kernel(tc, tab_words, tab_scales, offs, x, b, g
             listed_scales[:].bitcast(I32).rearrange("p (q t w) -> p t q w", t=4, w=2),
         )
 
-        weave_tokens(0)
-        gather_keys(0)
-        gather_values(1)
-        transpose_values(1)
-        finish_values(1)
         round_pairs(0)
-        gather_keys(1)
         gather_values(0)
         transpose_values(0)
+        round_pairs(1)
+        gather_values(1)
+        finish_values(0)
+        transpose_values(1)
+        gather_keys(0)
+        weave_tokens(0)
+        gather_keys(1)
         weave_tokens(1)
         weave_tokens(2)
-        weave_values(0)
+        weave_values(1)
         gather_keys(2)
-        quantise_values(0)
-        gather_values(2)
+        quantise_values(1)
         for a in range(S_PASSES):
             score_pass(a)
-        round_pairs(3)
-        transpose_values(2)
-        weave_values(2)
-        gather_values(3)
-        quantise_values(2)
-        for unit in range(3):
+        for unit in range(2):
             dense_passes(unit)
             mix_passes(unit)
-        transpose_values(3)
+        round_pairs(2)
+        gather_values(2)
+        transpose_values(2)
+        dense_passes(2)
+        round_pairs(3)
         add_residual(0)
-        for i in range(4, 8):
-            dense_tile(i)
-        round_pairs(5)
-        gather_values(4)
+        add_residual(1)
+        gather_values(3)
+        weave_values(2)
+        transpose_values(3)
+        quantise_values(2)
+        mix_passes(2)
+        dense_passes(3)
+        dense_passes(4)
+        round_pairs(4)
         gather_values(5)
+        gather_values(4)
+        add_residual(2)
+        gather_values(6)
         weave_values(3)
+        transpose_values(5)
+        weave_values(5)
         transpose_values(4)
         weave_values(4)
-        transpose_values(5)
-        for unit in range(3, 5):
-            quantise_values(unit)
-            mix_passes(unit)
-        round_pairs(7)
-        for unit in range(1, 4):
-            add_residual(unit)
-        for i in range(8, 12):
-            dense_tile(i)
-        add_residual(4)
-        gather_values(6)
-        gather_values(7)
-        weave_values(5)
         transpose_values(6)
         weave_values(6)
-        transpose_values(7)
-        for unit in range(5, 7):
+        dense_passes(5)
+        dense_passes(6)
+        for unit in (3, 5, 4, 6):
             quantise_values(unit)
             mix_passes(unit)
-        weave_values(7)
-        add_residual(5)
-        quantise_values(7)
-        add_residual(6)
-        mix_passes(7)
-        add_residual(7)
+        for unit in (3, 5, 4, 6):
+            add_residual(unit)
 
-        for i in range(N // P):
-            nc.sync.dma_start(out[P * i : P * (i + 1), :], residual[i])
+        for unit in (0, 1, 2, 3, 5, 4, 6):
+            for i in tiles_of(unit):
+                nc.sync.dma_start(out[P * i : P * (i + 1), :], residual[i])

@@ -165,16 +165,16 @@ def tile_list_paged_memory_layer_kernel(tc, tab_words, tab_scales, offs, x, b, g
                 pairs[unit] = keep.tile([P, 2 * T], BF16, name="pairs0", align_bytes=64)
             else:
                 pairs[unit] = placed("pairs%d" % unit, [P, 2 * T], BF16, *PAIRS_AT[unit])
-            dst = pairs[unit][:].rearrange("p (c e) -> p c e", e=2)
+            dst = pairs[unit][:].rearrange("p (c i e) -> p c e i", i=4, e=2)
             if unit == 0:
                 for side, half in enumerate(values[unit]):
-                    nc.scalar.copy(dst[:, T // 2 * side : T // 2 * (side + 1), :], half[:].rearrange("p e c -> p c e"))
+                    nc.scalar.copy(dst[:, T // 8 * side : T // 8 * (side + 1), :, :], half[:].rearrange("p e (c i) -> p c e i", i=4))
                 return
-            src = values[unit][:].rearrange("p e c -> p c e")
-            cut = GPSIMD_COLUMNS if unit >= 2 else 0
+            src = values[unit][:].rearrange("p e (c i) -> p c e i", i=4)
+            cut = GPSIMD_COLUMNS // 4 if unit >= 2 else 0
             if cut:
-                nc.gpsimd.tensor_copy(dst[:, 0:cut, :], src[:, 0:cut, :])
-            nc.scalar.copy(dst[:, cut:T, :], src[:, cut:T, :])
+                nc.gpsimd.tensor_copy(dst[:, 0:cut, :, :], src[:, 0:cut, :, :])
+            nc.scalar.copy(dst[:, cut : T // 4, :, :], src[:, cut : T // 4, :, :])
 
         def gather_values(unit):
             if UNIT_TILES[unit] == 1:

@@ -50,7 +50,6 @@ def tile_list_paged_memory_layer_kernel(tc, tab_words, tab_scales, offs, x, b, g
             return arena.tile(shape, dtype, name=name, offset=SLOT * slot + at, align_bytes=64)
 
         offsets = keep.tile([P, S // 16], U16, name="offsets")
-        nc.sync.dma_start(offsets[:], offs)
 
         key_scales = keep.tile([P, T], U8, name="key_scales", align_bytes=64)
         nc.gpsimd.memset(key_scales[:].bitcast(I32), 0)
@@ -69,6 +68,11 @@ def tile_list_paged_memory_layer_kernel(tc, tab_words, tab_scales, offs, x, b, g
         tokens, keys, values, residual = {}, {}, {}, {}
         x_q, picked, pairs, got, turned, values_q, woven_h, h_q, sums, banks = {}, {}, {}, {}, {}, {}, {}, {}, {}, {}
 
+        def load_small():
+            nc.sync.dma_start(offsets[:], offs)
+            for i, vec in enumerate((b, g)):
+                nc.sync.dma_start(bg_raw[S_PASSES * i : S_PASSES * (i + 1), :], vec.rearrange("(a j) -> a j", a=S_PASSES))
+
         def load_values(unit):
             tiles, first = UNIT_TILES[unit], FIRST_TILE[unit]
             if unit == 0:
@@ -78,6 +82,8 @@ def tile_list_paged_memory_layer_kernel(tc, tab_words, tab_scales, offs, x, b, g
                     rows = wdT[0 : 2 * P, T // 2 * side : T // 2 * (side + 1)]
                     nc.sync.dma_start(half[:], rows.rearrange("(p e) c -> p e c", e=2))
                     values[unit].append(half)
+                    if side == 0:
+                        load_small()
                 return
             values[unit] = placed("values%d" % unit, [P, tiles, T], F32, first)
             rows = wdT[P * first : P * (first + tiles), :]
@@ -111,8 +117,6 @@ def tile_list_paged_memory_layer_kernel(tc, tab_words, tab_scales, offs, x, b, g
                     w4_scales[:, s:16:4, :].rearrange("a q n -> q a n").bitcast(I32),
                 )
 
-        for i, vec in enumerate((b, g)):
-            nc.sync.dma_start(bg_raw[S_PASSES * i : S_PASSES * (i + 1), :], vec.rearrange("(a j) -> a j", a=S_PASSES))
         load_values(0)
         load_values(1)
         load_key_scales()
@@ -381,4 +385,5 @@ def tile_list_paged_memory_layer_kernel(tc, tab_words, tab_scales, offs, x, b, g
 
         for unit in (0, 1, 2, 3, 5, 4, 6):
             for i in tiles_of(unit):
-                nc.sync.dma_start(out[P * i : P * (i + 1), :], residual[i])
+                queue = nc.gpsimd if unit < 3 else nc.sync
+                queue.dma_start(out[P * i : P * (i + 1), :], residual[i])

@@ -105,7 +105,7 @@ def tile_list_paged_memory_layer_kernel(tc, tab_words, tab_scales, offs, x, b, g
 
         def load_key_scales():
             for quad in range(4):
-                nc.sync.dma_start(
+                nc.gpsimd.dma_start(
                     key_scales[32 * quad : 32 * quad + 4 * K_PASSES, :].bitcast(I32),
                     tab_scales[:, 4 * quad : 4 * quad + 4, :].bitcast(I32),
                 )
@@ -249,7 +249,10 @@ def tile_list_paged_memory_layer_kernel(tc, tab_words, tab_scales, offs, x, b, g
         def score_pass(a):
             active = placed("active%d" % a, [P, 4, M], F32, TOKEN_SLOT + 1 + a)
             for t in range(4):
-                bank = psum.tile([P, M], F32, name="sum", tag="sum", bufs=SUM_BANKS)
+                if 4 * a + t < SUM_BANKS:
+                    bank = psum.tile([P, M], F32, name="sum", tag="sum", bufs=SUM_BANKS)
+                else:
+                    bank = psum.tile([P, M], F32, name="turn", tag="turn", bufs=TURN_BANKS)
                 cols = slice(256 * t + P * a, 256 * t + P * (a + 1))
                 for k in range(K_PASSES):
                     nc.tensor.matmul_mx(
@@ -261,7 +264,10 @@ def tile_list_paged_memory_layer_kernel(tc, tab_words, tab_scales, offs, x, b, g
                         start=(k == 0),
                         stop=(k == K_PASSES - 1),
                     )
-                nc.scalar.activation(active[:, t, :], bank[:], ACT.Relu, bias=bg[:, t, a : a + 1])
+                if a == 0 and t >= 2:
+                    nc.vector.tensor_scalar(active[:, t, :], bank[:], bg[:, t, a : a + 1], 0.0, ALU.add, ALU.max)
+                else:
+                    nc.scalar.activation(active[:, t, :], bank[:], ACT.Relu, bias=bg[:, t, a : a + 1])
             woven_h[a] = placed("woven_h%d" % a, [P, 4 * M], BF16, TOKEN_SLOT, HALF * (1 - a))
             nc.vector.tensor_tensor(
                 woven_h[a][:].rearrange("p (c i t) -> p c t i", i=4, t=4),
@@ -385,5 +391,4 @@ def tile_list_paged_memory_layer_kernel(tc, tab_words, tab_scales, offs, x, b, g
 
         for unit in (0, 1, 2, 3, 5, 4, 6):
             for i in tiles_of(unit):
-                queue = nc.gpsimd if unit < 3 else nc.sync
-                queue.dma_start(out[P * i : P * (i + 1), :], residual[i])
+                nc.sync.dma_start(out[P * i : P * (i + 1), :], residual[i])

@@ -22,20 +22,20 @@ PASS = 4 * P
 K_PASSES = K // PASS
 S_PASSES = S // PASS
 SUM_BANKS, TURN_BANKS = 6, 2
-UNIT_TILES = (2, 2, 2, 2, 2, 1, 1)
+UNIT_TILES = (2, 1) * 4
 FIRST_TILE = tuple(sum(UNIT_TILES[:u]) for u in range(len(UNIT_TILES)))
+HALVED = (0, 6)
 
 SLOT = 8192
+HALF = SLOT // 2
 TOKEN_SLOT = N // P
 KEY_SLOT = TOKEN_SLOT + K_PASSES
 RESIDUAL_SLOT = KEY_SLOT + K_PASSES
 PICKED_SLOT = RESIDUAL_SLOT + 3
-HALF = SLOT // 2
-PAIRS_AT = {1: (0, 0), 2: (PICKED_SLOT, HALF), 3: (5, 0), 4: (7, 0)}
-GOT_AT = {0: (PICKED_SLOT + 1, HALF), 1: (1, 0), 2: (KEY_SLOT, 0), 3: (KEY_SLOT, HALF), 4: (KEY_SLOT + 1, 0), 5: (KEY_SLOT + 1, HALF), 6: (KEY_SLOT + 2, 0)}
-TURNED_AT = {0: (2, 0), 1: (TOKEN_SLOT + 2, 0), 2: (6, 0), 3: (8, 0), 4: (0, 0), 5: (3, 0), 6: (3, 2048)}
-CODES_AT = {0: (1, HALF), 1: (2, HALF), 2: (4, HALF), 3: (6, HALF), 4: (8, HALF), 5: (10, HALF), 6: (11, HALF)}
-GPSIMD_COLUMNS = 0
+PAIRS_AT = {0: PICKED_SLOT + 2, 2: KEY_SLOT, 4: KEY_SLOT + 1, 6: KEY_SLOT + 2}
+GOT_AT = {0: (0, 0), 1: (1, 0), 2: (3, 0), 3: (1, 2048), 4: (7, 0), 5: (1, HALF), 6: (9, 0), 7: (10, 2048)}
+TURNED_AT = {0: (TOKEN_SLOT, 0), 1: (2, 0), 2: (6, 0), 3: (5, 0), 4: (10, 0), 5: (8, 0), 6: (9, HALF), 7: (11, 0)}
+CODES_AT = {0: 0, 1: 2, 2: 4, 3: 5, 4: 7, 5: 8, 6: 10, 7: 11}
 
 
 def tile_list_paged_memory_layer_kernel(tc, tab_words, tab_scales, offs, x, b, g, wdT, w4_words, w4_scales, r, out):
@@ -59,13 +59,11 @@ def tile_list_paged_memory_layer_kernel(tc, tab_words, tab_scales, offs, x, b, g
         nc.vector.memset(bg_rows[:], 0.0)
         ident = keep.tile([P, P], F32, name="ident")
         make_identity(nc, ident[:])
-        ident16 = keep.tile([P, P], BF16, name="ident16")
-        make_identity(nc, ident16[:])
         dense = keep.tile([P, K_PASSES, 2 * N], U8, name="dense", align_bytes=64)
         bg = keep.tile([P, 4, 2 * S_PASSES], F32, name="bg")
         bg_raw = keep.tile([2 * S_PASSES, PASS], F32, name="bg_raw")
         picked_scales = keep.tile([P, S], U8, name="picked_scales", align_bytes=64)
-        tokens, keys, values, residual = {}, {}, {}, {}
+        tokens, keys, values, residual, scores, active = {}, {}, {}, {}, {}, {}
         x_q, picked, pairs, got, turned, values_q, woven_h, h_q, sums, banks = {}, {}, {}, {}, {}, {}, {}, {}, {}, {}
 
         def load_small():
@@ -75,19 +73,15 @@ def tile_list_paged_memory_layer_kernel(tc, tab_words, tab_scales, offs, x, b, g
 
         def load_values(unit):
             tiles, first = UNIT_TILES[unit], FIRST_TILE[unit]
-            if unit == 0:
-                values[unit] = []
-                for side in range(2):
-                    half = placed("values0_%d" % side, [P, 2, T // 2], F32, side)
-                    rows = wdT[0 : 2 * P, T // 2 * side : T // 2 * (side + 1)]
-                    nc.sync.dma_start(half[:], rows.rearrange("(p e) c -> p e c", e=2))
-                    values[unit].append(half)
-                    if side == 0:
-                        load_small()
-                return
-            values[unit] = placed("values%d" % unit, [P, tiles, T], F32, first)
-            rows = wdT[P * first : P * (first + tiles), :]
-            nc.sync.dma_start(values[unit][:], rows.rearrange("(p e) c -> p e c", e=tiles))
+            rows = wdT[P * first : P * (first + tiles), :].rearrange("(p e) c -> p e c", e=tiles)
+            parts = 2 if unit in HALVED else 1
+            values[unit] = []
+            for side in range(parts):
+                part = placed("values%d_%d" % (unit, side), [P, tiles, T // parts], F32, first + side)
+                nc.sync.dma_start(part[:], rows[:, :, T // parts * side : T // parts * (side + 1)])
+                values[unit].append(part)
+                if unit == 0 and side == 0:
+                    load_small()
 
         def load_tokens(a):
             tokens[a] = placed("tokens%d" % a, [P, 4, M], F32, TOKEN_SLOT + a)
@@ -106,7 +100,7 @@ def tile_list_paged_memory_layer_kernel(tc, tab_words, tab_scales, offs, x, b, g
         def load_key_scales():
             for quad in range(4):
                 nc.gpsimd.dma_start(
-                    key_scales[32 * quad : 32 * quad + 4 * K_PASSES, :].bitcast(I32),
+                    key_scales[32 * quad + 4 : 32 * quad + 4 + 4 * K_PASSES, :].bitcast(I32),
                     tab_scales[:, 4 * quad : 4 * quad + 4, :].bitcast(I32),
                 )
 
@@ -118,7 +112,6 @@ def tile_list_paged_memory_layer_kernel(tc, tab_words, tab_scales, offs, x, b, g
                 )
 
         load_values(0)
-        load_values(1)
         load_key_scales()
         load_dense_scales()
         load_keys(0)
@@ -127,14 +120,16 @@ def tile_list_paged_memory_layer_kernel(tc, tab_words, tab_scales, offs, x, b, g
         load_tokens(1)
         load_tokens(2)
         load_keys(2)
-        load_values(2)
+        load_values(1)
         nc.sync.dma_start(dense[:].bitcast(I32), w4_words.rearrange("a p n -> p a n").bitcast(I32))
-        load_values(3)
-        load_residual(0, 4)
+        load_values(2)
         load_values(4)
+        load_values(3)
+        load_residual(0, 3)
         load_values(5)
-        load_residual(4, 6)
         load_values(6)
+        load_residual(3, 6)
+        load_values(7)
         load_residual(6, 9)
         load_residual(9, 12)
 
@@ -165,41 +160,32 @@ def tile_list_paged_memory_layer_kernel(tc, tab_words, tab_scales, offs, x, b, g
             return [[dst[:, P * t : P * (t + 1)] for t in range(4)] for dst in parts]
 
         def round_pairs(unit):
-            if unit == 0:
-                pairs[unit] = keep.tile([P, 2 * T], BF16, name="pairs0", align_bytes=64)
-            else:
-                pairs[unit] = placed("pairs%d" % unit, [P, 2 * T], BF16, *PAIRS_AT[unit])
+            pairs[unit] = placed("pairs%d" % unit, [P, 2 * T], BF16, PAIRS_AT[unit])
             dst = pairs[unit][:].rearrange("p (c i e) -> p c e i", i=4, e=2)
-            if unit == 0:
-                for side, half in enumerate(values[unit]):
-                    nc.scalar.copy(dst[:, T // 8 * side : T // 8 * (side + 1), :, :], half[:].rearrange("p e (c i) -> p c e i", i=4))
-                return
-            src = values[unit][:].rearrange("p e (c i) -> p c e i", i=4)
-            cut = GPSIMD_COLUMNS // 4 if unit >= 2 else 0
-            if cut:
-                nc.gpsimd.tensor_copy(dst[:, 0:cut, :, :], src[:, 0:cut, :, :])
-            nc.scalar.copy(dst[:, cut : T // 4, :, :], src[:, cut : T // 4, :, :])
+            share = T // 4 // len(values[unit])
+            for side, part in enumerate(values[unit]):
+                nc.scalar.copy(dst[:, share * side : share * (side + 1), :, :], part[:].rearrange("p e (c i) -> p c e i", i=4))
 
         def gather_values(unit):
             if UNIT_TILES[unit] == 1:
                 dst = placed("got%d" % unit, [P, S], BF16, *GOT_AT[unit])
-                nc.vector.tensor_copy(in_list_layout(dst), values[unit][:, 0, :].indirect(offsets[:]))
-                got[unit] = [[dst[:, 256 * t + P * a : 256 * t + P * (a + 1)] for t in range(4)] for a in range(S_PASSES)]
+                nc.vector.tensor_copy(
+                    dst[:].rearrange("p (u q r e) -> p q u e r", u=2, r=8, e=2), values[unit][0][:, 0, :].indirect(offsets[:])
+                )
+                words = dst[:].bitcast(F32)
+                got[unit] = [[words[:, 256 * u + P * a : 256 * u + P * (a + 1)] for u in range(2)] for a in range(S_PASSES)]
                 return
-            if unit == 4:
-                parts = [placed("got%d_%d" % (unit, a), [P, PASS], U32, GOT_AT[unit][0], 4 * PASS * a) for a in range(S_PASSES)]
-            else:
-                parts = [placed("got%d" % unit, [P, S], U32, *GOT_AT[unit])]
+            parts = [placed("got%d" % unit, [P, S], U32, *GOT_AT[unit])]
             got[unit] = gather_words(pairs[unit][:].bitcast(U32), parts)
 
         def transpose_values(unit):
             tag, bufs = "turn", TURN_BANKS
             if UNIT_TILES[unit] == 1:
-                bank = psum.tile([P, S_PASSES, 4, P], BF16, name=tag, tag=tag, bufs=bufs)
+                bank = psum.tile([P, S_PASSES, 2, P], F32, name=tag, tag=tag, bufs=bufs)
                 for a in range(S_PASSES):
-                    for t in range(4):
-                        nc.tensor.transpose(bank[:, a, t, :], got[unit][a][t], ident16[:])
-                banks[unit] = [bank[:].rearrange("p a t n -> p (a t n)")]
+                    for u in range(2):
+                        nc.tensor.transpose(bank[:, a, u, :], got[unit][a][u], ident[:])
+                banks[unit] = [bank[:]]
                 return
             banks[unit] = []
             for a in range(S_PASSES):
@@ -215,8 +201,8 @@ def tile_list_paged_memory_layer_kernel(tc, tab_words, tab_scales, offs, x, b, g
                 flat = placed("turned%d_%d" % (unit, n), [P, S], BF16, slot, at + 2 * S * n)
                 if UNIT_TILES[unit] == 1:
                     nc.scalar.copy(
-                        flat[:].rearrange("p (a n t) -> p a n t", a=S_PASSES, t=4),
-                        bank.rearrange("p (a t n) -> p a n t", a=S_PASSES, t=4),
+                        flat[:].bitcast(F32).rearrange("p (a n u) -> p a n u", a=S_PASSES, u=2),
+                        bank.rearrange("p a u n -> p a n u"),
                     )
                 else:
                     nc.scalar.copy(flat[:].rearrange("p (n t) -> p n t", t=4), bank.rearrange("p (t n) -> p n t", t=4))
@@ -224,7 +210,7 @@ def tile_list_paged_memory_layer_kernel(tc, tab_words, tab_scales, offs, x, b, g
 
         def quantise_values(unit):
             for n, flat in enumerate(turned[unit]):
-                slot, at = CODES_AT[unit]
+                slot, at = CODES_AT[unit], HALF
                 codes, scales = quantise(flat[:], "values%d_%d" % (unit, n), slot, at + 5 * 2 * P * n)
                 for half in range(2):
                     cols = slice(P * half, P * (half + 1))
@@ -246,32 +232,35 @@ def tile_list_paged_memory_layer_kernel(tc, tab_words, tab_scales, offs, x, b, g
                 parts = [placed("picked%d_%d" % (k, a), [P, PASS], U32, PICKED_SLOT + 1, 4 * PASS * a) for a in range(S_PASSES)]
             picked[k] = gather_words(keys[k][:].bitcast(U32), parts)
 
-        def score_pass(a):
-            active = placed("active%d" % a, [P, 4, M], F32, TOKEN_SLOT + 1 + a)
-            for t in range(4):
-                if 4 * a + t < SUM_BANKS:
-                    bank = psum.tile([P, M], F32, name="sum", tag="sum", bufs=SUM_BANKS)
-                else:
-                    bank = psum.tile([P, M], F32, name="turn", tag="turn", bufs=TURN_BANKS)
-                cols = slice(256 * t + P * a, 256 * t + P * (a + 1))
-                for k in range(K_PASSES):
+        def score_passes(k):
+            for a in range(S_PASSES):
+                for t in range(4):
+                    if k == 0:
+                        if 4 <= 4 * a + t < 4 + TURN_BANKS:
+                            scores[a, t] = psum.tile([P, M], F32, name="turn", tag="turn", bufs=TURN_BANKS)
+                        else:
+                            scores[a, t] = psum.tile([P, M], F32, name="sum", tag="sum", bufs=SUM_BANKS)
+                    cols = slice(256 * t + P * a, 256 * t + P * (a + 1))
                     nc.tensor.matmul_mx(
-                        out=bank[:],
+                        out=scores[a, t][:],
                         lhsT=picked[k][a][t].bitcast(FP8X4),
-                        lhsT_scale=picked_scales[4 * k : P, cols],
+                        lhsT_scale=picked_scales[4 * (k + 1) : P, cols],
                         rhs=x_q[k][0][:].bitcast(FP8X4),
                         rhs_scale=x_q[k][1][:],
                         start=(k == 0),
                         stop=(k == K_PASSES - 1),
                     )
-                if a == 0 and t >= 2:
-                    nc.vector.tensor_scalar(active[:, t, :], bank[:], bg[:, t, a : a + 1], 0.0, ALU.add, ALU.max)
-                else:
-                    nc.scalar.activation(active[:, t, :], bank[:], ACT.Relu, bias=bg[:, t, a : a + 1])
+
+        def activate(a):
+            active[a] = placed("active%d" % a, [P, 4, M], F32, TOKEN_SLOT + 1 + a)
+            for t in range(4):
+                nc.scalar.activation(active[a][:, t, :], scores[a, t][:], ACT.Relu, bias=bg[:, t, a : a + 1])
+
+        def gain(a):
             woven_h[a] = placed("woven_h%d" % a, [P, 4 * M], BF16, TOKEN_SLOT, HALF * (1 - a))
             nc.vector.tensor_tensor(
                 woven_h[a][:].rearrange("p (c i t) -> p c t i", i=4, t=4),
-                active[:].rearrange("p t (c i) -> p c t i", i=4),
+                active[a][:].rearrange("p t (c i) -> p c t i", i=4),
                 bg[:, :, S_PASSES + a : S_PASSES + a + 1].unsqueeze(1).to_broadcast([P, M // 4, 4, 4]),
                 ALU.mult,
             )
@@ -311,13 +300,19 @@ def tile_list_paged_memory_layer_kernel(tc, tab_words, tab_scales, offs, x, b, g
                         stop=(a == S_PASSES - 1),
                     )
 
-        def add_residual(unit):
-            for i in tiles_of(unit):
+        def add_residual(tiles):
+            for i in tiles:
                 nc.vector.tensor_tensor(residual[i], sums[i][:], residual[i], ALU.add)
 
-        def finish_values(unit):
+        def turn(unit):
+            transpose_values(unit)
             weave_values(unit)
-            quantise_values(unit)
+
+        def multiply(units):
+            for unit in units:
+                dense_passes(unit)
+            for unit in units:
+                mix_passes(unit)
 
         nc.scalar.copy(
             bg_rows[0 : 2 * S_PASSES, :].rearrange("p (t q r) -> p t q r", t=4, r=8),
@@ -337,58 +332,52 @@ def tile_list_paged_memory_layer_kernel(tc, tab_words, tab_scales, offs, x, b, g
 
         round_pairs(0)
         gather_values(0)
-        transpose_values(0)
-        round_pairs(1)
-        gather_values(1)
-        finish_values(0)
-        transpose_values(1)
         gather_keys(0)
         weave_tokens(0)
+        turn(0)
         gather_keys(1)
         weave_tokens(1)
         weave_tokens(2)
-        weave_values(1)
         gather_keys(2)
-        quantise_values(1)
-        for a in range(S_PASSES):
-            score_pass(a)
-        for unit in range(2):
-            dense_passes(unit)
-            mix_passes(unit)
+        for k in range(K_PASSES):
+            score_passes(k)
+        activate(0)
+        gather_values(1)
+        activate(1)
+        gain(0)
+        gain(1)
+        turn(1)
         round_pairs(2)
+        quantise_values(0)
+        quantise_values(1)
         gather_values(2)
-        transpose_values(2)
-        dense_passes(2)
-        round_pairs(3)
-        add_residual(0)
-        add_residual(1)
         gather_values(3)
-        weave_values(2)
-        transpose_values(3)
-        quantise_values(2)
-        mix_passes(2)
-        dense_passes(3)
-        dense_passes(4)
         round_pairs(4)
-        gather_values(5)
         gather_values(4)
-        add_residual(2)
-        gather_values(6)
-        weave_values(3)
-        transpose_values(5)
-        weave_values(5)
+        turn(2)
+        turn(3)
         transpose_values(4)
+        multiply((0, 1))
+        quantise_values(2)
+        quantise_values(3)
+        multiply((2, 3))
+        add_residual(range(0, 3))
+        gather_values(5)
+        round_pairs(6)
+        gather_values(6)
         weave_values(4)
-        transpose_values(6)
-        weave_values(6)
-        dense_passes(5)
-        dense_passes(6)
-        for unit in (3, 5, 4, 6):
-            quantise_values(unit)
-            mix_passes(unit)
-        for unit in (3, 5, 4, 6):
-            add_residual(unit)
+        turn(5)
+        add_residual(range(3, 6))
+        quantise_values(4)
+        quantise_values(5)
+        gather_values(7)
+        turn(6)
+        turn(7)
+        multiply((4, 5))
+        quantise_values(6)
+        quantise_values(7)
+        multiply((6, 7))
+        add_residual(range(6, 12))
 
-        for unit in (0, 1, 2, 3, 5, 4, 6):
-            for i in tiles_of(unit):
-                nc.sync.dma_start(out[P * i : P * (i + 1), :], residual[i])
+        for i in range(N // P):
+            nc.sync.dma_start(out[P * i : P * (i + 1), :], residual[i])

@@ -24,7 +24,9 @@ S_PASSES = S // PASS
 SUM_BANKS, TURN_BANKS = 6, 2
 UNIT_TILES = (2, 1) * 4
 FIRST_TILE = tuple(sum(UNIT_TILES[:u]) for u in range(len(UNIT_TILES)))
-HALVED = (0, 6)
+HALVED = (0, 2, 4, 6)
+VECTOR_WEAVES = ()
+FIRST_IN_TURN_BANK = 6
 
 SLOT = 8192
 HALF = SLOT // 2
@@ -33,9 +35,9 @@ KEY_SLOT = TOKEN_SLOT + K_PASSES
 RESIDUAL_SLOT = KEY_SLOT + K_PASSES
 PICKED_SLOT = RESIDUAL_SLOT + 3
 PAIRS_AT = {0: PICKED_SLOT + 2, 2: KEY_SLOT, 4: KEY_SLOT + 1, 6: KEY_SLOT + 2}
-GOT_AT = {0: (0, 0), 1: (1, 0), 2: (3, 0), 3: (1, 2048), 4: (7, 0), 5: (1, HALF), 6: (9, 0), 7: (10, 2048)}
-TURNED_AT = {0: (TOKEN_SLOT, 0), 1: (2, 0), 2: (6, 0), 3: (5, 0), 4: (10, 0), 5: (8, 0), 6: (9, HALF), 7: (11, 0)}
-CODES_AT = {0: 0, 1: 2, 2: 4, 3: 5, 4: 7, 5: 8, 6: 10, 7: 11}
+GOT_AT = {0: (0, 0), 1: (1, 0), 2: (3, 0), 3: (1, 2048), 4: (6, 0), 5: (1, HALF), 6: (9, 0), 7: (9, HALF + 2048)}
+TURNED_AT = {0: ((TOKEN_SLOT + 2, 0), (TOKEN_SLOT + 2, 2048)), 1: ((2, 0),), 2: ((7, 0), (7, 2048)), 3: ((5, 0),), 4: ((9, HALF), (9, HALF + 2048)), 5: ((8, 0),), 6: ((3, HALF), (3, HALF + 2048)), 7: ((11, 0),)}
+CODES_AT = {0: KEY_SLOT + 2, 1: 2, 2: 4, 3: 5, 4: 6, 5: 8, 6: 10, 7: 11}
 
 
 def tile_list_paged_memory_layer_kernel(tc, tab_words, tab_scales, offs, x, b, g, wdT, w4_words, w4_scales, r, out):
@@ -52,7 +54,7 @@ def tile_list_paged_memory_layer_kernel(tc, tab_words, tab_scales, offs, x, b, g
         offsets = keep.tile([P, S // 16], U16, name="offsets")
 
         key_scales = keep.tile([P, T], U8, name="key_scales", align_bytes=64)
-        nc.gpsimd.memset(key_scales[:].bitcast(I32), 0)
+        nc.vector.memset(key_scales[:].bitcast(I32), 0)
         dense_scales = keep.tile([P, K_PASSES, N], U8, name="dense_scales", align_bytes=64)
         nc.vector.memset(dense_scales[:].rearrange("p a n -> p (a n)").bitcast(I32), 0)
         bg_rows = keep.tile([P, PASS], F32, name="bg_rows")
@@ -66,22 +68,17 @@ def tile_list_paged_memory_layer_kernel(tc, tab_words, tab_scales, offs, x, b, g
         tokens, keys, values, residual, scores, active = {}, {}, {}, {}, {}, {}
         x_q, picked, pairs, got, turned, values_q, woven_h, h_q, sums, banks = {}, {}, {}, {}, {}, {}, {}, {}, {}, {}
 
-        def load_small():
-            nc.sync.dma_start(offsets[:], offs)
+        def load_bias_gain():
             for i, vec in enumerate((b, g)):
                 nc.sync.dma_start(bg_raw[S_PASSES * i : S_PASSES * (i + 1), :], vec.rearrange("(a j) -> a j", a=S_PASSES))
 
-        def load_values(unit):
+        def load_values(unit, side=0):
             tiles, first = UNIT_TILES[unit], FIRST_TILE[unit]
             rows = wdT[P * first : P * (first + tiles), :].rearrange("(p e) c -> p e c", e=tiles)
-            parts = 2 if unit in HALVED else 1
-            values[unit] = []
-            for side in range(parts):
-                part = placed("values%d_%d" % (unit, side), [P, tiles, T // parts], F32, first + side)
-                nc.sync.dma_start(part[:], rows[:, :, T // parts * side : T // parts * (side + 1)])
-                values[unit].append(part)
-                if unit == 0 and side == 0:
-                    load_small()
+            width = T // 2 if unit in HALVED else T
+            part = placed("values%d_%d" % (unit, side), [P, tiles, width], F32, first + side)
+            nc.sync.dma_start(part[:], rows[:, :, width * side : width * (side + 1)])
+            values.setdefault(unit, []).append(part)
 
         def load_tokens(a):
             tokens[a] = placed("tokens%d" % a, [P, 4, M], F32, TOKEN_SLOT + a)
@@ -99,35 +96,41 @@ def tile_list_paged_memory_layer_kernel(tc, tab_words, tab_scales, offs, x, b, g
 
         def load_key_scales():
             for quad in range(4):
-                nc.gpsimd.dma_start(
+                nc.sync.dma_start(
                     key_scales[32 * quad + 4 : 32 * quad + 4 + 4 * K_PASSES, :].bitcast(I32),
                     tab_scales[:, 4 * quad : 4 * quad + 4, :].bitcast(I32),
                 )
 
         def load_dense_scales():
             for s in range(4):
-                nc.gpsimd.dma_start(
+                nc.sync.dma_start(
                     dense_scales[s:P:32, :, :].bitcast(I32),
                     w4_scales[:, s:16:4, :].rearrange("a q n -> q a n").bitcast(I32),
                 )
 
         load_values(0)
-        load_key_scales()
-        load_dense_scales()
+        nc.sync.dma_start(offsets[:], offs)
         load_keys(0)
+        load_key_scales()
+        load_bias_gain()
+        load_values(0, 1)
         load_tokens(0)
         load_keys(1)
         load_tokens(1)
         load_tokens(2)
         load_keys(2)
         load_values(1)
+        load_dense_scales()
         nc.sync.dma_start(dense[:].bitcast(I32), w4_words.rearrange("a p n -> p a n").bitcast(I32))
         load_values(2)
-        load_values(4)
+        load_values(2, 1)
         load_values(3)
+        load_values(4)
+        load_values(4, 1)
         load_residual(0, 3)
         load_values(5)
         load_values(6)
+        load_values(6, 1)
         load_residual(3, 6)
         load_values(7)
         load_residual(6, 9)
@@ -195,10 +198,9 @@ def tile_list_paged_memory_layer_kernel(tc, tab_words, tab_scales, offs, x, b, g
                 banks[unit].append(bank[:].rearrange("p t n -> p (t n)").bitcast(BF16))
 
         def weave_values(unit):
-            slot, at = TURNED_AT[unit]
             turned[unit] = []
             for n, bank in enumerate(banks[unit]):
-                flat = placed("turned%d_%d" % (unit, n), [P, S], BF16, slot, at + 2 * S * n)
+                flat = placed("turned%d_%d" % (unit, n), [P, S], BF16, *TURNED_AT[unit][n])
                 if UNIT_TILES[unit] == 1:
                     nc.scalar.copy(
                         flat[:].bitcast(F32).rearrange("p (a n u) -> p a n u", a=S_PASSES, u=2),
@@ -219,7 +221,7 @@ def tile_list_paged_memory_layer_kernel(tc, tab_words, tab_scales, offs, x, b, g
 
         def weave_tokens(a):
             woven_x = woven_tile()
-            nc.scalar.copy(
+            (nc.vector.tensor_copy if a in VECTOR_WEAVES else nc.scalar.copy)(
                 woven_x[:].rearrange("p (c i t) -> p c t i", i=4, t=4),
                 tokens[a][:].rearrange("p t (c i) -> p c t i", i=4),
             )
@@ -236,7 +238,7 @@ def tile_list_paged_memory_layer_kernel(tc, tab_words, tab_scales, offs, x, b, g
             for a in range(S_PASSES):
                 for t in range(4):
                     if k == 0:
-                        if 4 <= 4 * a + t < 4 + TURN_BANKS:
+                        if FIRST_IN_TURN_BANK <= 4 * a + t < FIRST_IN_TURN_BANK + TURN_BANKS:
                             scores[a, t] = psum.tile([P, M], F32, name="turn", tag="turn", bufs=TURN_BANKS)
                         else:
                             scores[a, t] = psum.tile([P, M], F32, name="sum", tag="sum", bufs=SUM_BANKS)
@@ -318,7 +320,7 @@ def tile_list_paged_memory_layer_kernel(tc, tab_words, tab_scales, offs, x, b, g
             bg_rows[0 : 2 * S_PASSES, :].rearrange("p (t q r) -> p t q r", t=4, r=8),
             bg_raw[:].rearrange("p (q t r) -> p t q r", t=4, r=8),
         )
-        bg_bank = psum.tile([P, 4, P], F32, name="turn", tag="turn", bufs=TURN_BANKS)
+        bg_bank = psum.tile([P, 4, P], F32, name="sum", tag="sum", bufs=SUM_BANKS)
         for t in range(4):
             nc.tensor.transpose(bg_bank[:, t, :], bg_rows[:, P * t : P * (t + 1)], ident[:])
         nc.scalar.copy(bg[:], bg_bank[:, :, 0 : 2 * S_PASSES])

@@ -22,11 +22,12 @@ PASS = 4 * P
 K_PASSES = K // PASS
 S_PASSES = S // PASS
 SUM_BANKS, TURN_BANKS = 6, 2
-UNIT_TILES = (2, 1) * 4
+UNIT_TILES = (2, 1, 1, 1, 2, 1, 2, 1, 1)
 FIRST_TILE = tuple(sum(UNIT_TILES[:u]) for u in range(len(UNIT_TILES)))
-HALVED = (0, 2, 4, 6)
+HALVED = (0,)
 VECTOR_WEAVES = ()
 FIRST_IN_TURN_BANK = 6
+GPSIMD_TILES = 6
 
 SLOT = 8192
 HALF = SLOT // 2
@@ -34,10 +35,11 @@ TOKEN_SLOT = N // P
 KEY_SLOT = TOKEN_SLOT + K_PASSES
 RESIDUAL_SLOT = KEY_SLOT + K_PASSES
 PICKED_SLOT = RESIDUAL_SLOT + 3
-PAIRS_AT = {0: PICKED_SLOT + 2, 2: KEY_SLOT, 4: KEY_SLOT + 1, 6: KEY_SLOT + 2}
-GOT_AT = {0: (0, 0), 1: (1, 0), 2: (3, 0), 3: (1, 2048), 4: (6, 0), 5: (1, HALF), 6: (9, 0), 7: (9, HALF + 2048)}
-TURNED_AT = {0: ((TOKEN_SLOT + 2, 0), (TOKEN_SLOT + 2, 2048)), 1: ((2, 0),), 2: ((7, 0), (7, 2048)), 3: ((5, 0),), 4: ((9, HALF), (9, HALF + 2048)), 5: ((8, 0),), 6: ((3, HALF), (3, HALF + 2048)), 7: ((11, 0),)}
-CODES_AT = {0: KEY_SLOT + 2, 1: 2, 2: 4, 3: 5, 4: 6, 5: 8, 6: 10, 7: 11}
+PAIRS_AT = {0: PICKED_SLOT + 2, 4: KEY_SLOT, 6: KEY_SLOT + 1}
+GOT_AT = {0: (0, 0), 1: (1, 0), 2: (TOKEN_SLOT + 2, HALF), 3: (1, HALF), 4: (5, 0), 5: (1, HALF + 2048), 6: (2, 0), 7: (0, HALF), 8: (0, HALF + 2048)}
+TURNED_AT = {0: ((TOKEN_SLOT + 2, 0), (TOKEN_SLOT + 2, 2048)), 1: ((2, 0),), 2: ((6, 0),), 3: ((6, 2048),), 4: ((9, 0), (9, 2048)), 5: ((7, 0),), 6: ((PICKED_SLOT + 1, HALF), (PICKED_SLOT + 1, HALF + 2048)), 7: ((10, 0),), 8: ((11, 0),)}
+CODES_AT = {0: (KEY_SLOT + 2, HALF), 1: (2, HALF), 2: (3, HALF), 3: (4, HALF), 4: (3, 0), 5: (7, HALF), 6: (4, 0), 7: (10, HALF), 8: (11, HALF)}
+MIXED_AT = ((6, HALF), (8, 0), (8, 2048), (8, HALF), (8, HALF + 2048), (PICKED_SLOT + 1, 2048), (PICKED_SLOT + 1, 4096), (PICKED_SLOT + 1, 6144))
 
 
 def tile_list_paged_memory_layer_kernel(tc, tab_words, tab_scales, offs, x, b, g, wdT, w4_words, w4_scales, r, out):
@@ -65,7 +67,7 @@ def tile_list_paged_memory_layer_kernel(tc, tab_words, tab_scales, offs, x, b, g
         bg = keep.tile([P, 4, 2 * S_PASSES], F32, name="bg")
         bg_raw = keep.tile([2 * S_PASSES, PASS], F32, name="bg_raw")
         picked_scales = keep.tile([P, S], U8, name="picked_scales", align_bytes=64)
-        tokens, keys, values, residual, scores, active = {}, {}, {}, {}, {}, {}
+        tokens, keys, values, residual, scores, active, mixed = {}, {}, {}, {}, {}, {}, {}
         x_q, picked, pairs, got, turned, values_q, woven_h, h_q, sums, banks = {}, {}, {}, {}, {}, {}, {}, {}, {}, {}
 
         def load_bias_gain():
@@ -123,18 +125,15 @@ def tile_list_paged_memory_layer_kernel(tc, tab_words, tab_scales, offs, x, b, g
         load_dense_scales()
         nc.sync.dma_start(dense[:].bitcast(I32), w4_words.rearrange("a p n -> p a n").bitcast(I32))
         load_values(2)
-        load_values(2, 1)
-        load_values(3)
         load_values(4)
-        load_values(4, 1)
-        load_residual(0, 3)
-        load_values(5)
+        load_values(3)
         load_values(6)
-        load_values(6, 1)
-        load_residual(3, 6)
+        load_values(5)
+        load_residual(0, 4)
         load_values(7)
-        load_residual(6, 9)
-        load_residual(9, 12)
+        load_values(8)
+        load_residual(4, 8)
+        load_residual(8, 12)
 
         def quantise(src, name, slot=None, at=0):
             width = src.shape[1] // 4
@@ -212,7 +211,7 @@ def tile_list_paged_memory_layer_kernel(tc, tab_words, tab_scales, offs, x, b, g
 
         def quantise_values(unit):
             for n, flat in enumerate(turned[unit]):
-                slot, at = CODES_AT[unit], HALF
+                slot, at = CODES_AT[unit]
                 codes, scales = quantise(flat[:], "values%d_%d" % (unit, n), slot, at + 5 * 2 * P * n)
                 for half in range(2):
                     cols = slice(P * half, P * (half + 1))
@@ -302,9 +301,17 @@ def tile_list_paged_memory_layer_kernel(tc, tab_words, tab_scales, offs, x, b, g
                         stop=(a == S_PASSES - 1),
                     )
 
+        def empty_banks(tiles):
+            for i in tiles:
+                mixed[i] = placed("mixed%d" % i, [P, M], F32, *MIXED_AT[i])
+                nc.scalar.copy(mixed[i][:], sums[i][:])
+
         def add_residual(tiles):
             for i in tiles:
-                nc.vector.tensor_tensor(residual[i], sums[i][:], residual[i], ALU.add)
+                if i < GPSIMD_TILES:
+                    nc.gpsimd.tensor_tensor(residual[i], mixed[i][:], residual[i], ALU.add)
+                else:
+                    nc.vector.tensor_tensor(residual[i], sums[i][:], residual[i], ALU.add)
 
         def turn(unit):
             transpose_values(unit)
@@ -349,37 +356,58 @@ def tile_list_paged_memory_layer_kernel(tc, tab_words, tab_scales, offs, x, b, g
         gain(0)
         gain(1)
         turn(1)
-        round_pairs(2)
         quantise_values(0)
         quantise_values(1)
-        gather_values(2)
-        gather_values(3)
+        dense_tile(0)
+        dense_tile(1)
+        dense_tile(2)
+        mix_passes(0)
+        mix_passes(1)
+        dense_tile(3)
+        dense_tile(4)
+        dense_tile(5)
         round_pairs(4)
-        gather_values(4)
+        gather_values(2)
         turn(2)
+        gather_values(3)
+        empty_banks((0, 1,))
         turn(3)
+        gather_values(4)
         transpose_values(4)
-        multiply((0, 1))
         quantise_values(2)
-        quantise_values(3)
-        multiply((2, 3))
-        add_residual(range(0, 3))
-        gather_values(5)
+        mix_passes(2)
+        dense_tile(6)
+        dense_tile(7)
         round_pairs(6)
+        gather_values(5)
         gather_values(6)
+        quantise_values(3)
+        mix_passes(3)
         weave_values(4)
-        turn(5)
-        add_residual(range(3, 6))
-        quantise_values(4)
-        quantise_values(5)
+        empty_banks((2, 3, 4,))
         gather_values(7)
+        turn(5)
+        quantise_values(4)
+        mix_passes(4)
         turn(6)
+        dense_tile(8)
+        dense_tile(9)
+        dense_tile(10)
+        gather_values(8)
+        quantise_values(5)
+        mix_passes(5)
+        empty_banks((5,))
         turn(7)
-        multiply((4, 5))
+        turn(8)
+        dense_tile(11)
+        add_residual((0, 1, 2, 3,))
         quantise_values(6)
         quantise_values(7)
-        multiply((6, 7))
-        add_residual(range(6, 12))
+        quantise_values(8)
+        mix_passes(6)
+        mix_passes(7)
+        mix_passes(8)
+        add_residual((4, 5, 6, 7, 8, 9, 10, 11,))
 
         for i in range(N // P):
             nc.sync.dma_start(out[P * i : P * (i + 1), :], residual[i])

@@ -28,6 +28,7 @@ HALVED = (0,)
 VECTOR_WEAVES = ()
 FIRST_IN_TURN_BANK = 6
 GPSIMD_TILES = 6
+SCALAR_GAIN_TOKENS = (0, 384)
 
 SLOT = 8192
 HALF = SLOT // 2
@@ -259,12 +260,22 @@ def tile_list_paged_memory_layer_kernel(tc, tab_words, tab_scales, offs, x, b, g
 
         def gain(a):
             woven_h[a] = placed("woven_h%d" % a, [P, 4 * M], BF16, TOKEN_SLOT, HALF * (1 - a))
+            own = M - SCALAR_GAIN_TOKENS[a]
+            gains = bg[:, :, S_PASSES + a : S_PASSES + a + 1]
             nc.vector.tensor_tensor(
-                woven_h[a][:].rearrange("p (c i t) -> p c t i", i=4, t=4),
-                active[a][:].rearrange("p t (c i) -> p c t i", i=4),
-                bg[:, :, S_PASSES + a : S_PASSES + a + 1].unsqueeze(1).to_broadcast([P, M // 4, 4, 4]),
+                woven_h[a][:, 0 : 4 * own].rearrange("p (c i t) -> p c t i", i=4, t=4),
+                active[a][:, :, 0:own].rearrange("p t (c i) -> p c t i", i=4),
+                gains.unsqueeze(1).to_broadcast([P, own // 4, 4, 4]),
                 ALU.mult,
             )
+            if own < M:
+                gained = placed("gained", [P, 4, M - own], BF16, KEY_SLOT + 2)
+                for t in range(4):
+                    nc.scalar.activation(gained[:, t, :], active[a][:, t, own:M], ACT.Copy, scale=gains[:, t, :])
+                nc.vector.tensor_copy(
+                    woven_h[a][:, 4 * own : 4 * M].rearrange("p (c i t) -> p c t i", i=4, t=4),
+                    gained[:].rearrange("p t (c i) -> p c t i", i=4),
+                )
             h_q[a] = quantise(woven_h[a][:], "h%d" % a, TOKEN_SLOT + 1 + a)
 
         def tiles_of(unit):

@@ -64,7 +64,7 @@ def tile_list_paged_memory_layer_kernel(tc, tab_words, tab_scales, offs, x, b, g
         nc.vector.memset(bg_rows[:], 0.0)
         ident = keep.tile([P, P], F32, name="ident")
         make_identity(nc, ident[:])
-        dense = keep.tile([P, K_PASSES, 2 * N], U8, name="dense", align_bytes=64)
+        dense = [keep.tile([P, K_PASSES, N], U8, name="dense%d" % half, align_bytes=64) for half in range(2)]
         bg = keep.tile([P, 4, 2 * S_PASSES], F32, name="bg")
         bg_raw = keep.tile([2 * S_PASSES, PASS], F32, name="bg_raw")
         picked_scales = keep.tile([P, S], U8, name="picked_scales", align_bytes=64)
@@ -104,6 +104,10 @@ def tile_list_paged_memory_layer_kernel(tc, tab_words, tab_scales, offs, x, b, g
                     tab_scales[:, 4 * quad : 4 * quad + 4, :].bitcast(I32),
                 )
 
+        def load_dense(half):
+            columns = w4_words[:, :, N * half : N * (half + 1)].rearrange("a p n -> p a n")
+            nc.sync.dma_start(dense[half][:].bitcast(I32), columns.bitcast(I32))
+
         def load_dense_scales():
             for s in range(4):
                 nc.sync.dma_start(
@@ -124,12 +128,13 @@ def tile_list_paged_memory_layer_kernel(tc, tab_words, tab_scales, offs, x, b, g
         load_keys(2)
         load_values(1)
         load_dense_scales()
-        nc.sync.dma_start(dense[:].bitcast(I32), w4_words.rearrange("a p n -> p a n").bitcast(I32))
+        load_dense(0)
         load_values(2)
         load_values(4)
         load_values(3)
         load_values(6)
         load_values(5)
+        load_dense(1)
         load_residual(0, 4)
         load_values(7)
         load_values(8)
@@ -286,7 +291,7 @@ def tile_list_paged_memory_layer_kernel(tc, tab_words, tab_scales, offs, x, b, g
             for k in range(K_PASSES):
                 nc.tensor.matmul_mx(
                     out=sums[i][:],
-                    lhsT=dense[:, k, 2 * P * i : 2 * P * (i + 1)].bitcast(FP4X4),
+                    lhsT=dense[i // 6][:, k, 2 * P * (i % 6) : 2 * P * (i % 6 + 1)].bitcast(FP4X4),
                     lhsT_scale=dense_scales[:, k, P * i : P * (i + 1)],
                     rhs=x_q[k][0][:].bitcast(FP8X4),
                     rhs_scale=x_q[k][1][:],

@@ -39,7 +39,7 @@ PICKED_SLOT = RESIDUAL_SLOT + 3
 PAIRS_AT = {0: PICKED_SLOT + 2, 4: KEY_SLOT, 6: KEY_SLOT + 1}
 GOT_AT = {0: (0, 0), 1: (1, 0), 2: (TOKEN_SLOT + 2, HALF), 3: (1, HALF), 4: (5, 0), 5: (1, HALF + 2048), 6: (2, 0), 7: (0, HALF), 8: (0, HALF + 2048)}
 TURNED_AT = {0: ((TOKEN_SLOT + 2, 0), (TOKEN_SLOT + 2, 2048)), 1: ((2, 0),), 2: ((6, 0),), 3: ((6, 2048),), 4: ((9, 0), (9, 2048)), 5: ((7, 0),), 6: ((PICKED_SLOT + 1, HALF), (PICKED_SLOT + 1, HALF + 2048)), 7: ((10, 0),), 8: ((11, 0),)}
-CODES_AT = {0: (KEY_SLOT + 2, HALF), 1: (2, HALF), 2: (3, HALF), 3: (4, HALF), 4: (3, 0), 5: (7, HALF), 6: (4, 0), 7: (10, HALF), 8: (11, HALF)}
+CODES_AT = {0: (KEY_SLOT + 2, HALF), 1: (2, HALF), 2: (3, HALF), 3: (4, HALF), 4: (3, 0), 5: (11, 2048), 6: (11, 5632), 7: (10, HALF), 8: (11, HALF)}
 MIXED_AT = ((6, HALF), (8, 0), (8, 2048), (8, HALF), (8, HALF + 2048), (PICKED_SLOT + 1, 2048), (PICKED_SLOT + 1, 4096), (PICKED_SLOT + 1, 6144))
 
 
@@ -99,7 +99,7 @@ def tile_list_paged_memory_layer_kernel(tc, tab_words, tab_scales, offs, x, b, g
 
         def load_key_scales():
             for quad in range(4):
-                nc.sync.dma_start(
+                nc.gpsimd.dma_start(
                     key_scales[32 * quad + 4 : 32 * quad + 4 + 4 * K_PASSES, :].bitcast(I32),
                     tab_scales[:, 4 * quad : 4 * quad + 4, :].bitcast(I32),
                 )
@@ -137,9 +137,10 @@ def tile_list_paged_memory_layer_kernel(tc, tab_words, tab_scales, offs, x, b, g
         load_dense(1)
         load_residual(0, 4)
         load_values(7)
+        load_residual(4, 6)
         load_values(8)
-        load_residual(4, 8)
-        load_residual(8, 12)
+        load_residual(6, 9)
+        load_residual(9, 12)
 
         def quantise(src, name, slot=None, at=0):
             width = src.shape[1] // 4

from contextlib import ExitStack

import concourse.mybir as mybir
from concourse.masks import make_identity

K, T, S, M, N = 1536, 2048, 1024, 512, 1536
FLOPS = 2 * M * (K * S + S * N + K * N)

F32 = mybir.dt.float32
BF16 = mybir.dt.bfloat16
I32 = mybir.dt.int32
U32 = mybir.dt.uint32
U16 = mybir.dt.uint16
U8 = mybir.dt.uint8
FP8X4 = mybir.dt.float8_e4m3fn_x4
FP4X4 = mybir.dt.float4_e2m1fn_x4
ACT = mybir.ActivationFunctionType
ALU = mybir.AluOpType

P = 128
PASS = 4 * P
K_PASSES = K // PASS
S_PASSES = S // PASS
SUM_BANKS, TURN_BANKS = 6, 2
UNIT_TILES = (2, 1, 1, 1, 2, 1, 2, 1, 1)
FIRST_TILE = tuple(sum(UNIT_TILES[:u]) for u in range(len(UNIT_TILES)))
HALVED = (0,)
VECTOR_WEAVES = ()
FIRST_IN_TURN_BANK = 6
GPSIMD_TILES = 6
SCALAR_GAIN_TOKENS = (0, 384)

SLOT = 8192
HALF = SLOT // 2
TOKEN_SLOT = N // P
KEY_SLOT = TOKEN_SLOT + K_PASSES
RESIDUAL_SLOT = KEY_SLOT + K_PASSES
PICKED_SLOT = RESIDUAL_SLOT + 3
PAIRS_AT = {0: PICKED_SLOT + 2, 4: KEY_SLOT, 6: KEY_SLOT + 1}
GOT_AT = {0: (0, 0), 1: (1, 0), 2: (TOKEN_SLOT + 2, HALF), 3: (1, HALF), 4: (5, 0), 5: (1, HALF + 2048), 6: (2, 0), 7: (0, HALF), 8: (0, HALF + 2048)}
TURNED_AT = {0: ((TOKEN_SLOT + 2, 0), (TOKEN_SLOT + 2, 2048)), 1: ((2, 0),), 2: ((6, 0),), 3: ((6, 2048),), 4: ((9, 0), (9, 2048)), 5: ((7, 0),), 6: ((PICKED_SLOT + 1, HALF), (PICKED_SLOT + 1, HALF + 2048)), 7: ((10, 0),), 8: ((11, 0),)}
CODES_AT = {0: (KEY_SLOT + 2, HALF), 1: (2, HALF), 2: (3, HALF), 3: (4, HALF), 4: (3, 0), 5: (11, 2048), 6: (11, 5632), 7: (10, HALF), 8: (11, HALF)}
MIXED_AT = ((6, HALF), (8, 0), (8, 2048), (8, HALF), (8, HALF + 2048), (PICKED_SLOT + 1, 2048), (PICKED_SLOT + 1, 4096), (PICKED_SLOT + 1, 6144))


def tile_list_paged_memory_layer_kernel(tc, tab_words, tab_scales, offs, x, b, g, wdT, w4_words, w4_scales, r, out):
    nc = tc.nc
    with ExitStack() as ctx:
        keep = ctx.enter_context(tc.tile_pool(name="keep", bufs=1))
        arena = ctx.enter_context(tc.tile_pool(name="arena", bufs=1))
        ring = ctx.enter_context(tc.tile_pool(name="ring", bufs=2))
        psum = ctx.enter_context(tc.psum_pool(name="psum", bufs=1))

        def placed(name, shape, dtype, slot, at=0):
            return arena.tile(shape, dtype, name=name, offset=SLOT * slot + at, align_bytes=64)

        offsets = keep.tile([P, S // 16], U16, name="offsets")

        key_scales = keep.tile([P, T], U8, name="key_scales", align_bytes=64)
        nc.vector.memset(key_scales[:].bitcast(I32), 0)
        dense_scales = keep.tile([P, K_PASSES, N], U8, name="dense_scales", align_bytes=64)
        nc.vector.memset(dense_scales[:].rearrange("p a n -> p (a n)").bitcast(I32), 0)
        bg_rows = keep.tile([P, PASS], F32, name="bg_rows")
        nc.vector.memset(bg_rows[:], 0.0)
        ident = keep.tile([P, P], F32, name="ident")
        make_identity(nc, ident[:])
        dense = [keep.tile([P, K_PASSES, N], U8, name="dense%d" % half, align_bytes=64) for half in range(2)]
        bg = keep.tile([P, 4, 2 * S_PASSES], F32, name="bg")
        bg_raw = keep.tile([2 * S_PASSES, PASS], F32, name="bg_raw")
        picked_scales = keep.tile([P, S], U8, name="picked_scales", align_bytes=64)
        tokens, keys, values, residual, scores, active, mixed = {}, {}, {}, {}, {}, {}, {}
        x_q, picked, pairs, got, turned, values_q, woven_h, h_q, sums, banks = {}, {}, {}, {}, {}, {}, {}, {}, {}, {}

        def load_bias_gain():
            for i, vec in enumerate((b, g)):
                nc.sync.dma_start(bg_raw[S_PASSES * i : S_PASSES * (i + 1), :], vec.rearrange("(a j) -> a j", a=S_PASSES))

        def load_values(unit, side=0):
            tiles, first = UNIT_TILES[unit], FIRST_TILE[unit]
            rows = wdT[P * first : P * (first + tiles), :].rearrange("(p e) c -> p e c", e=tiles)
            width = T // 2 if unit in HALVED else T
            part = placed("values%d_%d" % (unit, side), [P, tiles, width], F32, first + side)
            nc.sync.dma_start(part[:], rows[:, :, width * side : width * (side + 1)])
            values.setdefault(unit, []).append(part)

        def load_tokens(a):
            tokens[a] = placed("tokens%d" % a, [P, 4, M], F32, TOKEN_SLOT + a)
            nc.sync.dma_start(tokens[a][:], x[PASS * a : PASS * (a + 1), :].rearrange("(p t) m -> p t m", t=4))

        def load_keys(a):
            keys[a] = placed("keys%d" % a, [P, T], I32, KEY_SLOT + a)
            nc.sync.dma_start(keys[a][:], tab_words[a].rearrange("p n t -> p (n t)").bitcast(I32))

        def load_residual(first, stop):
            tile = placed("residual%d" % first, [P, stop - first, M], F32, RESIDUAL_SLOT, 4 * M * first)
            nc.sync.dma_start(tile[:], r[P * first : P * stop, :].rearrange("(i p) m -> p i m", p=P))
            for i in range(first, stop):
                residual[i] = tile[:, i - first, :]

        def load_key_scales():
            for quad in range(4):
                nc.gpsimd.dma_start(
                    key_scales[32 * quad + 4 : 32 * quad + 4 + 4 * K_PASSES, :].bitcast(I32),
                    tab_scales[:, 4 * quad : 4 * quad + 4, :].bitcast(I32),
                )

        def load_dense(half):
            columns = w4_words[:, :, N * half : N * (half + 1)].rearrange("a p n -> p a n")
            nc.sync.dma_start(dense[half][:].bitcast(I32), columns.bitcast(I32))

        def load_dense_scales():
            for s in range(4):
                nc.sync.dma_start(
                    dense_scales[s:P:32, :, :].bitcast(I32),
                    w4_scales[:, s:16:4, :].rearrange("a q n -> q a n").bitcast(I32),
                )

        load_values(0)
        nc.sync.dma_start(offsets[:], offs)
        load_keys(0)
        load_key_scales()
        load_bias_gain()
        load_values(0, 1)
        load_tokens(0)
        load_keys(1)
        load_tokens(1)
        load_tokens(2)
        load_keys(2)
        load_values(1)
        load_dense_scales()
        load_dense(0)
        load_values(2)
        load_values(4)
        load_values(3)
        load_values(6)
        load_values(5)
        load_dense(1)
        load_residual(0, 4)
        load_values(7)
        load_residual(4, 6)
        load_values(8)
        load_residual(6, 9)
        load_residual(9, 12)

        def quantise(src, name, slot=None, at=0):
            width = src.shape[1] // 4
            if slot is None:
                codes = keep.tile([P, width], U32, name=name + "_codes", align_bytes=64)
                scales = keep.tile([P, width], U8, name=name + "_scales", align_bytes=64)
            else:
                codes = placed(name + "_codes", [P, width], U32, slot, at)
                scales = placed(name + "_scales", [P, width], U8, slot, at + 4 * width)
            nc.vector.quantize_mx(out=codes[:].bitcast(FP8X4), scales=scales[:], in_=src)
            return codes, scales

        def woven_tile():
            return ring.tile([P, 4 * M], BF16, name="woven", tag="woven", bufs=2, align_bytes=64)

        def in_list_layout(tile):
            return tile[:].rearrange("p (t q r) -> p q t r", t=4, r=8)

        def gather_words(window, parts):
            if len(parts) == 1:
                dst = parts[0]
                nc.vector.tensor_copy(in_list_layout(dst), window.indirect(offsets[:]))
                return [[dst[:, 256 * t + P * a : 256 * t + P * (a + 1)] for t in range(4)] for a in range(S_PASSES)]
            for a, dst in enumerate(parts):
                nc.vector.tensor_copy(in_list_layout(dst), window.indirect(offsets[:, 32 * a : 32 * (a + 1)]))
            return [[dst[:, P * t : P * (t + 1)] for t in range(4)] for dst in parts]

        def round_pairs(unit):
            pairs[unit] = placed("pairs%d" % unit, [P, 2 * T], BF16, PAIRS_AT[unit])
            dst = pairs[unit][:].rearrange("p (c i e) -> p c e i", i=4, e=2)
            share = T // 4 // len(values[unit])
            for side, part in enumerate(values[unit]):
                nc.scalar.copy(dst[:, share * side : share * (side + 1), :, :], part[:].rearrange("p e (c i) -> p c e i", i=4))

        def gather_values(unit):
            if UNIT_TILES[unit] == 1:
                dst = placed("got%d" % unit, [P, S], BF16, *GOT_AT[unit])
                nc.vector.tensor_copy(
                    dst[:].rearrange("p (u q r e) -> p q u e r", u=2, r=8, e=2), values[unit][0][:, 0, :].indirect(offsets[:])
                )
                words = dst[:].bitcast(F32)
                got[unit] = [[words[:, 256 * u + P * a : 256 * u + P * (a + 1)] for u in range(2)] for a in range(S_PASSES)]
                return
            parts = [placed("got%d" % unit, [P, S], U32, *GOT_AT[unit])]
            got[unit] = gather_words(pairs[unit][:].bitcast(U32), parts)

        def transpose_values(unit):
            tag, bufs = "turn", TURN_BANKS
            if UNIT_TILES[unit] == 1:
                bank = psum.tile([P, S_PASSES, 2, P], F32, name=tag, tag=tag, bufs=bufs)
                for a in range(S_PASSES):
                    for u in range(2):
                        nc.tensor.transpose(bank[:, a, u, :], got[unit][a][u], ident[:])
                banks[unit] = [bank[:]]
                return
            banks[unit] = []
            for a in range(S_PASSES):
                bank = psum.tile([P, 4, P], F32, name=tag, tag=tag, bufs=bufs)
                for t in range(4):
                    nc.tensor.transpose(bank[:, t, :], got[unit][a][t].bitcast(F32), ident[:])
                banks[unit].append(bank[:].rearrange("p t n -> p (t n)").bitcast(BF16))

        def weave_values(unit):
            turned[unit] = []
            for n, bank in enumerate(banks[unit]):
                flat = placed("turned%d_%d" % (unit, n), [P, S], BF16, *TURNED_AT[unit][n])
                if UNIT_TILES[unit] == 1:
                    nc.scalar.copy(
                        flat[:].bitcast(F32).rearrange("p (a n u) -> p a n u", a=S_PASSES, u=2),
                        bank.rearrange("p a u n -> p a n u"),
                    )
                else:
                    nc.scalar.copy(flat[:].rearrange("p (n t) -> p n t", t=4), bank.rearrange("p (t n) -> p n t", t=4))
                turned[unit].append(flat)

        def quantise_values(unit):
            for n, flat in enumerate(turned[unit]):
                slot, at = CODES_AT[unit]
                codes, scales = quantise(flat[:], "values%d_%d" % (unit, n), slot, at + 5 * 2 * P * n)
                for half in range(2):
                    cols = slice(P * half, P * (half + 1))
                    key = (FIRST_TILE[unit] + half, n) if UNIT_TILES[unit] == 2 else (FIRST_TILE[unit], half)
                    values_q[key] = codes[:, cols], scales[:, cols]

        def weave_tokens(a):
            woven_x = woven_tile()
            (nc.vector.tensor_copy if a in VECTOR_WEAVES else nc.scalar.copy)(
                woven_x[:].rearrange("p (c i t) -> p c t i", i=4, t=4),
                tokens[a][:].rearrange("p t (c i) -> p c t i", i=4),
            )
            x_q[a] = quantise(woven_x[:], "x%d" % a)

        def gather_keys(k):
            if k + 1 < K_PASSES:
                parts = [placed("picked%d" % k, [P, S], U32, PICKED_SLOT, HALF * k)]
            else:
                parts = [placed("picked%d_%d" % (k, a), [P, PASS], U32, PICKED_SLOT + 1, 4 * PASS * a) for a in range(S_PASSES)]
            picked[k] = gather_words(keys[k][:].bitcast(U32), parts)

        def score_passes(k):
            for a in range(S_PASSES):
                for t in range(4):
                    if k == 0:
                        if FIRST_IN_TURN_BANK <= 4 * a + t < FIRST_IN_TURN_BANK + TURN_BANKS:
                            scores[a, t] = psum.tile([P, M], F32, name="turn", tag="turn", bufs=TURN_BANKS)
                        else:
                            scores[a, t] = psum.tile([P, M], F32, name="sum", tag="sum", bufs=SUM_BANKS)
                    cols = slice(256 * t + P * a, 256 * t + P * (a + 1))
                    nc.tensor.matmul_mx(
                        out=scores[a, t][:],
                        lhsT=picked[k][a][t].bitcast(FP8X4),
                        lhsT_scale=picked_scales[4 * (k + 1) : P, cols],
                        rhs=x_q[k][0][:].bitcast(FP8X4),
                        rhs_scale=x_q[k][1][:],
                        start=(k == 0),
                        stop=(k == K_PASSES - 1),
                    )

        def activate(a):
            active[a] = placed("active%d" % a, [P, 4, M], F32, TOKEN_SLOT + 1 + a)
            for t in range(4):
                nc.scalar.activation(active[a][:, t, :], scores[a, t][:], ACT.Relu, bias=bg[:, t, a : a + 1])

        def gain(a):
            woven_h[a] = placed("woven_h%d" % a, [P, 4 * M], BF16, TOKEN_SLOT, HALF * (1 - a))
            own = M - SCALAR_GAIN_TOKENS[a]
            gains = bg[:, :, S_PASSES + a : S_PASSES + a + 1]
            nc.vector.tensor_tensor(
                woven_h[a][:, 0 : 4 * own].rearrange("p (c i t) -> p c t i", i=4, t=4),
                active[a][:, :, 0:own].rearrange("p t (c i) -> p c t i", i=4),
                gains.unsqueeze(1).to_broadcast([P, own // 4, 4, 4]),
                ALU.mult,
            )
            if own < M:
                gained = placed("gained", [P, 4, M - own], BF16, KEY_SLOT + 2)
                for t in range(4):
                    nc.scalar.activation(gained[:, t, :], active[a][:, t, own:M], ACT.Copy, scale=gains[:, t, :])
                nc.vector.tensor_copy(
                    woven_h[a][:, 4 * own : 4 * M].rearrange("p (c i t) -> p c t i", i=4, t=4),
                    gained[:].rearrange("p t (c i) -> p c t i", i=4),
                )
            h_q[a] = quantise(woven_h[a][:], "h%d" % a, TOKEN_SLOT + 1 + a)

        def tiles_of(unit):
            return range(FIRST_TILE[unit], FIRST_TILE[unit] + UNIT_TILES[unit])

        def dense_tile(i):
            sums[i] = psum.tile([P, M], F32, name="sum", tag="sum", bufs=SUM_BANKS)
            for k in range(K_PASSES):
                nc.tensor.matmul_mx(
                    out=sums[i][:],
                    lhsT=dense[i // 6][:, k, 2 * P * (i % 6) : 2 * P * (i % 6 + 1)].bitcast(FP4X4),
                    lhsT_scale=dense_scales[:, k, P * i : P * (i + 1)],
                    rhs=x_q[k][0][:].bitcast(FP8X4),
                    rhs_scale=x_q[k][1][:],
                    start=(k == 0),
                    stop=False,
                )

        def dense_passes(unit):
            for i in tiles_of(unit):
                dense_tile(i)

        def mix_passes(unit):
            for a in range(S_PASSES):
                for i in tiles_of(unit):
                    codes, scales = values_q[i, a]
                    nc.tensor.matmul_mx(
                        out=sums[i][:],
                        lhsT=codes.bitcast(FP8X4),
                        lhsT_scale=scales,
                        rhs=h_q[a][0][:].bitcast(FP8X4),
                        rhs_scale=h_q[a][1][:],
                        start=False,
                        stop=(a == S_PASSES - 1),
                    )

        def empty_banks(tiles):
            for i in tiles:
                mixed[i] = placed("mixed%d" % i, [P, M], F32, *MIXED_AT[i])
                nc.scalar.copy(mixed[i][:], sums[i][:])

        def add_residual(tiles):
            for i in tiles:
                if i < GPSIMD_TILES:
                    nc.gpsimd.tensor_tensor(residual[i], mixed[i][:], residual[i], ALU.add)
                else:
                    nc.vector.tensor_tensor(residual[i], sums[i][:], residual[i], ALU.add)

        def turn(unit):
            transpose_values(unit)
            weave_values(unit)

        def multiply(units):
            for unit in units:
                dense_passes(unit)
            for unit in units:
                mix_passes(unit)

        nc.scalar.copy(
            bg_rows[0 : 2 * S_PASSES, :].rearrange("p (t q r) -> p t q r", t=4, r=8),
            bg_raw[:].rearrange("p (q t r) -> p t q r", t=4, r=8),
        )
        bg_bank = psum.tile([P, 4, P], F32, name="sum", tag="sum", bufs=SUM_BANKS)
        for t in range(4):
            nc.tensor.transpose(bg_bank[:, t, :], bg_rows[:, P * t : P * (t + 1)], ident[:])
        nc.scalar.copy(bg[:], bg_bank[:, :, 0 : 2 * S_PASSES])

        listed_scales = keep.tile([P, S], U8, name="listed_scales", align_bytes=64)
        nc.vector.tensor_copy(listed_scales[:], key_scales[:].indirect(offsets[:]))
        nc.vector.tensor_copy(
            picked_scales[:].bitcast(I32).rearrange("p (t q w) -> p t q w", t=4, w=2),
            listed_scales[:].bitcast(I32).rearrange("p (q t w) -> p t q w", t=4, w=2),
        )

        round_pairs(0)
        gather_values(0)
        gather_keys(0)
        weave_tokens(0)
        turn(0)
        gather_keys(1)
        weave_tokens(1)
        weave_tokens(2)
        gather_keys(2)
        for k in range(K_PASSES):
            score_passes(k)
        activate(0)
        gather_values(1)
        activate(1)
        gain(0)
        gain(1)
        turn(1)
        quantise_values(0)
        quantise_values(1)
        dense_tile(0)
        dense_tile(1)
        dense_tile(2)
        mix_passes(0)
        mix_passes(1)
        dense_tile(3)
        dense_tile(4)
        dense_tile(5)
        round_pairs(4)
        gather_values(2)
        turn(2)
        gather_values(3)
        empty_banks((0, 1,))
        turn(3)
        gather_values(4)
        transpose_values(4)
        quantise_values(2)
        mix_passes(2)
        dense_tile(6)
        dense_tile(7)
        round_pairs(6)
        gather_values(5)
        gather_values(6)
        quantise_values(3)
        mix_passes(3)
        weave_values(4)
        empty_banks((2, 3, 4,))
        gather_values(7)
        turn(5)
        quantise_values(4)
        mix_passes(4)
        turn(6)
        dense_tile(8)
        dense_tile(9)
        dense_tile(10)
        gather_values(8)
        quantise_values(5)
        mix_passes(5)
        empty_banks((5,))
        turn(7)
        turn(8)
        dense_tile(11)
        add_residual((0, 1, 2, 3,))
        quantise_values(6)
        quantise_values(7)
        quantise_values(8)
        mix_passes(6)
        mix_passes(7)
        mix_passes(8)
        add_residual((4, 5, 6, 7, 8, 9, 10, 11,))

        for i in range(N // P):
            nc.sync.dma_start(out[P * i : P * (i + 1), :], residual[i])
